import numpy as np
import ml_dtypes


def mxq(x, axis, fmt="e4m3"):
    dtype, down = {"e4m3": (ml_dtypes.float8_e4m3fn, 7), "e5m2": (ml_dtypes.float8_e5m2, 14)}[fmt]
    v = np.moveaxis(np.asarray(x, np.float32).astype(ml_dtypes.bfloat16).astype(np.float64), axis, -1)
    blocks = v.reshape(v.shape[:-1] + (-1, 32))
    amax = np.abs(blocks).max(-1, keepdims=True)
    byte = np.maximum(np.where(amax > 0, np.frexp(amax)[1] - 1 + 127, 0) - down, 1)
    scale = np.exp2(byte - 127.0)
    codes = (blocks / scale).astype(np.float32).astype(dtype).astype(np.float64)
    return np.moveaxis((codes * scale).reshape(v.shape), -1, axis)


WIDE = False


def mx_kscale(k):
    if not WIDE:
        return np.ones(k)
    levels = np.array([10, -10, 5, -5, 0])
    if k % 512:
        return np.exp2(np.random.permutation(np.resize(levels, k // 32))).repeat(32)
    a = np.empty((k // 512, 16))
    for p in range(k // 512):
        a[p, :8] = np.random.permutation(np.resize(levels, 8))
        for g in range(8):
            far = levels[np.abs(levels - a[p, g]) >= 10]
            a[p, g + 8] = far[np.random.randint(len(far))]
    return np.exp2(a.ravel()).repeat(32)


BF16 = ml_dtypes.bfloat16


def bf(x):
    return np.asarray(x, np.float32).astype(BF16)


def f64(x):
    return np.asarray(x).astype(np.float64)

E4M3FN = np.array([(-1.0 if i & 128 else 1.0) * ((1.0 + (i & 7) / 8.0) * 2.0 ** (((i >> 3) & 15) - 7) if i & 120 else (i & 7) * 2.0 ** -9) for i in range(256)])


def e4m3fn_bytes(y):
    return np.clip(np.asarray(y, np.float64), -448.0, 448.0).astype(np.float32).astype(ml_dtypes.float8_e4m3fn).view(np.uint8)


def e4m3fn_values(b):
    return E4M3FN[b]


P, C, F, N = 1024, 2048, 1024, 2048


def setup_inputs():
    s, t = mx_kscale(C), mx_kscale(F)
    w1 = np.random.standard_normal((C, F)) / np.sqrt(C) / s[:, None]
    w2 = 2 * np.random.standard_normal((F, N)) / np.sqrt(F) / t[:, None]
    w1_scale = (np.abs(w1).max(axis=1, keepdims=True) / 448).astype(np.float32)
    w2_scale = (np.abs(w2).max(axis=1, keepdims=True) / 448).astype(np.float32)
    return {"x": bf(np.random.standard_normal((P, C)) * s),
            "W1_bytes": e4m3fn_bytes(w1 / w1_scale),
            "W1_scale": w1_scale,
            "g": bf((1 + 0.1 * np.random.standard_normal(F)) * t),
            "W2_bytes": e4m3fn_bytes(w2 / w2_scale),
            "W2_scale": w2_scale,
            "b": bf(0.3 * np.random.standard_normal(N))}


def reference(x, W1_bytes, W1_scale, g, W2_bytes, W2_scale, b):
    w1 = e4m3fn_values(W1_bytes) * np.repeat(f64(W1_scale), F, axis=1)
    w2 = e4m3fn_values(W2_bytes) * np.repeat(f64(W2_scale), N, axis=1)
    y = mxq(f64(x), 1, "e4m3") @ mxq(w1, 0, "e4m3")
    h = y * f64(g)
    z = (mxq(h, 1, "e4m3") @ mxq(w2, 0, "e4m3")) + f64(b)
    return z * np.clip(z + 3, 0, 6) / 6

@@ -1,0 +1,294 @@
+from contextlib import ExitStack
+
+import concourse.mybir as mybir
+from concourse.masks import make_identity
+
+PIX, CIN, MID, COUT = 1024, 2048, 1024, 2048
+FLOPS = 2 * PIX * CIN * MID + 2 * PIX * MID * COUT
+
+F32 = mybir.dt.float32
+BF16 = mybir.dt.bfloat16
+U32 = mybir.dt.uint32
+U8 = mybir.dt.uint8
+FP8 = mybir.dt.float8_e4m3fn
+FP8X4 = mybir.dt.float8_e4m3fn_x4
+ALU = mybir.AluOpType
+ACT = mybir.ActivationFunctionType
+
+P = 128
+PACK = 4
+SPAN = P * PACK
+BANKS = 8
+
+DIRECT = ()
+OUTS = ((0, 0), (1, 0), (0, 1), (1, 1), (2, 0), (2, 1), (3, 0), (3, 1))
+ORDER = (
+    "widen.S.0.3 widen.V.0.2 widen.V.0.0 widen.S.0.1 widen.V.1.3 widen.S.1.1 widen.V.1.2 weave.V.0 widen.S.1.0 xturn.P.0.0 "
+    "weave.V.1 widen.S.2.2 xturn.P.0.1 xcopy.S.0.0 widen.S.2.3 widen.V.2.1 wq.V.0 xcopy.S.0.1 xturn.P.1.0 wq.V.1 "
+    "widen.S.2.0 xturn.P.1.1 xq.V.0 widen.S.3.2 xcopy.V.1.0 xcopy.S.1.1 widen.S.3.1 weave.V.2 widen.S.3.0 xturn.P.2.0 "
+    "xturn.P.2.1 widen.S.3.3 widen.V.4.1 widen.V.5.3 xcopy.S.2.0 wq.V.2 xcopy.S.2.1 weave.V.3 xturn.P.3.0 widen.S.5.1 "
+    "xturn.P.3.1 widen.S.5.2 xq.V.1 widen.S.6.0 widen.S.5.0 wq.V.3 widen.S.4.2 bcopy.V widen.V.6.3 mm1.P.0.0 "
+    "weave.V.5 widen.S.4.0 widen.S.4.3 xturn.P.4.1 widen.S.6.1 xq.V.2 xcopy.S.3.0 xturn.P.5.1 wq.V.5 xcopy.S.3.1 "
+    "xturn.P.4.0 weave.V.4 widen.S.7.3 xturn.P.6.0 widen.S.7.1 mm1.P.2.0 hs.V.0.0 widen.S.6.2 xq.V.3 xcopy.S.4.0 "
+    "xturn.P.5.0 weave.V.6 xcopy.S.4.1 mm1.P.1.0 widen.S.7.2 widen.S.9.0 wq.V.4 widen.S.7.0 mm1.P.3.0 xq.V.4 "
+    "xcopy.S.5.0 wq.V.6 widen.S.8.3 weave.V.7 bturn.P xcopy.S.5.1 xcopy.S.6.0 xturn.P.6.1 hs.V.2.0 widen.S.9.2 "
+    "xturn.P.7.1 wq.V.7 widen.S.9.1 xturn.P.7.0 hs.V.3.0 widen.S.9.3 mm1.P.1.1 xq.V.5 xcopy.S.6.1 hs.V.1.0 "
+    "widen.S.11.2 weave.V.9 mm1.P.2.1 widen.S.8.1 widen.S.8.0 widen.S.10.2 mm1.P.3.1 hq.V.0.0 widen.S.8.2 hs.V.2.1 "
+    "bcol.S widen.S.10.1 mm1.P.0.1 xq.V.6 xcopy.S.7.0 weave.V.8 widen.S.11.1 mm1.P.5.1 widen.S.10.0 hs.V.1.1 "
+    "xcopy.S.7.1 mm1.P.4.0 wq.V.8 widen.S.11.3 hs.V.0.1 widen.S.13.3 hs.V.3.1 mm1.P.6.0 widen.S.10.3 wq.V.9 "
+    "widen.S.13.2 hq.V.0.1 widen.S.12.3 mm1.P.4.1 xq.V.7 widen.S.13.1 weave.V.10 widen.S.11.0 mm2.P.0.3 mm2.P.0.2 "
+    "bias.S.0.3 mm2.P.0.1 hs.V.5.1 widen.S.12.1 mm2.P.0.0 hs.V.6.0 bias.S.0.1 mm1.P.6.1 hs.V.4.0 widen.S.14.0 "
+    "hs.V.4.1 widen.S.14.3 weave.V.11 mm1.P.7.0 bias.S.0.2 widen.S.13.0 mm1.P.5.0 hs.V.6.1 bias.S.0.0 wq.V.11 "
+    "widen.S.12.2 wq.V.10 mm1.P.7.1 widen.S.12.0 hs.V.5.0 widen.S.15.0 hs.V.7.0 widen.S.14.2 mm2.P.1.3 hs.V.7.1 "
+    "widen.S.14.1 mm2.P.1.1 weave.V.13 bias.S.1.3 mm2.P.1.2 mm2.P.1.0 bias.S.1.1 turn.P.0.3 hq.V.1.1 bias.S.1.2 "
+    "turn.P.0.0 hq.V.1.0 gate.S.0.3 turn.P.0.1 turn.P.0.2 widen.V.15.1 gate.S.0.0 mm2.P.2.3 weave.V.12 bias.S.1.0 "
+    "mm2.P.2.0 gate.S.0.1 mm2.P.2.1 fin.V.0.3 gate.S.0.2 turn.P.1.0 fin.V.0.0 store.D.0.3 bias.S.2.0 mm2.P.2.2 "
+    "widen.V.15.3 fin.V.0.1 gate.S.1.0 turn.P.1.3 fin.V.0.2 bias.S.2.3 mm2.P.3.2 store.D.0.1 store.D.0.0 fin.V.1.0 "
+    "bias.S.2.1 turn.P.1.1 bias.V.2.2 gate.S.1.3 store.D.1.0 turn.P.1.2 wq.V.12 mm2.P.3.3 gate.S.1.1 wq.V.13 "
+    "mm2.P.3.0 gate.S.1.2 fin.V.1.1 mm2.P.3.1 bias.S.3.2 fin.V.1.3 mm2.P.4.1 bias.S.3.0 widen.V.15.2 bias.S.3.3 "
+    "turn.P.2.0 store.D.1.3 fin.V.1.2 store.D.0.2 store.D.1.1 turn.P.2.1 weave.V.14 bias.S.3.1 turn.P.2.2 store.D.1.2 "
+    "turn.P.2.3 gate.S.2.0 mm2.P.4.0 gate.S.2.1 weave.V.15 mm2.P.4.3 bias.S.4.1 mm2.P.5.2 gate.S.2.2 mm2.P.4.2 "
+    "fin.V.2.0 gate.S.2.3 fin.V.2.1 bias.S.4.0 turn.P.3.1 fin.V.2.2 turn.P.3.0 store.D.2.1 bias.S.4.3 fin.V.2.3 "
+    "turn.P.3.2 gate.S.3.0 wq.V.15 turn.P.3.3 store.D.2.3 store.D.2.0 gate.S.3.1 store.D.2.2 bias.V.4.2 mm2.P.5.3 "
+    "bias.S.5.2 wq.V.14 mm2.P.5.0 gate.S.3.2 fin.V.3.1 turn.P.4.1 gate.S.3.3 fin.V.3.0 turn.P.4.3 store.D.3.1 "
+    "mm2.P.5.1 bias.S.5.3 fin.V.3.2 store.D.3.0 mm2.P.6.3 gate.S.4.1 fin.V.3.3 turn.P.4.2 bias.V.5.1 bias.S.5.0 "
+    "store.D.3.3 turn.P.4.0 fin.V.4.1 gate.S.4.3 mm2.P.6.1 bias.V.6.3 gate.S.4.2 mm2.P.6.0 fin.V.4.3 gate.S.4.0 "
+    "mm2.P.6.2 bias.V.6.1 bias.S.6.0 store.D.4.3 turn.P.5.1 store.D.4.1 store.D.3.2 fin.V.4.2 turn.P.5.3 gate.S.5.1 "
+    "turn.P.5.0 fin.V.4.0 store.D.4.2 mm2.P.7.0 gate.S.5.3 bias.V.6.2 store.D.4.0 turn.P.5.2 fin.V.5.1 gate.S.5.0 "
+    "turn.P.6.1 fin.V.5.3 gate.S.5.2 turn.P.6.3 store.D.5.1 mm2.P.7.2 fin.V.5.0 gate.S.6.1 mm2.P.7.1 bias.V.7.0 "
+    "gate.S.6.3 store.D.5.0 mm2.P.7.3 fin.V.6.1 bias.S.7.2 turn.P.6.0 fin.V.5.2 bias.S.7.1 store.D.6.1 store.D.5.3 "
+    "turn.P.6.2 bias.V.7.3 gate.S.6.0 store.D.5.2 fin.V.6.3 gate.S.6.2 turn.P.7.1 turn.P.7.3 fin.V.6.0 store.D.6.3 "
+    "gate.S.7.1 turn.P.7.0 fin.V.6.2 turn.P.7.2 gate.S.7.3 store.D.6.0 fin.V.7.1 store.D.6.2 gate.S.7.0 fin.V.7.3 "
+    "gate.S.7.2 store.D.7.1 fin.V.7.0 store.D.7.3 fin.V.7.2 store.D.7.0 store.D.7.2 "
+)
+FAST = False
+
+
+def tile_pointwise_bottleneck_hardswish_d5_kernel(tc, x, W1_bytes, W1_scale, g, W2_bytes, W2_scale, b, out):
+    nc = tc.nc
+    with ExitStack() as ctx:
+        keep = ctx.enter_context(tc.tile_pool(name="keep", bufs=1))
+        psum = ctx.enter_context(tc.psum_pool(name="psum", bufs=1))
+        ctx.enter_context(tc.manual_schedule())
+
+        filled = []
+
+        def next_bank(shape):
+            bank = psum.tile(shape, F32, name="bank%d" % (len(filled) % BANKS))
+            filled.append(bank)
+            return bank
+
+        def ring(kind, n, depth, shape, dtype):
+            return keep.tile(shape, dtype, name="%s%d" % (kind, n % depth), align_bytes=64)
+
+        ident = keep.tile([P, P], F32, name="ident")
+        s1 = keep.tile([P, CIN // SPAN, PACK], F32, name="s1")
+        s2 = keep.tile([P, MID // SPAN, PACK], F32, name="s2")
+        g_sb = keep.tile([P, MID // SPAN, PACK], BF16, name="g_sb")
+        b_rows = keep.tile([COUT // P, P], BF16, name="b_rows")
+        b_sq = keep.tile([P, P], F32, name="b_sq")
+        b_col = keep.tile([P, COUT // P], F32, name="b_col")
+        half = keep.tile([P, 1], F32, name="half")
+        warm = keep.tile([P, 1], F32, name="warm")
+
+        pieces = [(1, k, c) for c in range(2) for k in range(4)] + [(2, k, c) for c in range(4) for k in range(2)]
+        raw, wide, woven, w_codes, w_scales = {}, {}, {}, {}, {}
+        x_sb, x_banks, x_woven, x_codes, x_scales = {}, {}, {}, {}, {}
+        y_bank, h_woven, h_codes, h_scales = {}, {}, {}, {}
+        zt_bank, zt_sb, z_src, gate_sb, b_wide = {}, {}, {}, {}, {}
+
+        def load_piece(u):
+            which, k, c = pieces[u]
+            src = W1_bytes if which == 1 else W2_bytes
+            raw[u] = keep.tile([P, PACK, SPAN], U8, name="raw%d" % u, align_bytes=64)
+            nc.sync.dma_start(
+                out=raw[u][:],
+                in_=src[k * SPAN : (k + 1) * SPAN, c * SPAN : (c + 1) * SPAN].rearrange("(p j) n -> p j n", j=PACK),
+            )
+
+        def load_x(i):
+            x_sb[i] = keep.tile([P, CIN], BF16, name="x%d" % i, align_bytes=64)
+            nc.sync.dma_start(out=x_sb[i][:], in_=x[i * P : (i + 1) * P, :])
+
+        def load_b_wide(c):
+            b_wide[c] = keep.tile([P, SPAN], BF16, name="b_wide%d" % c, align_bytes=64)
+            nc.sync.dma_start(out=b_wide[c][:], in_=b[c * SPAN : (c + 1) * SPAN].partition_broadcast(P))
+
+        def widen(on, u, j):
+            which, k, c = pieces[u]
+            scale = (s1 if which == 1 else s2)[:, k, j : j + 1]
+            if u not in wide:
+                wide[u] = ring("wide", u, 4, [P, PACK, SPAN], BF16)
+            src = raw[u][:, j, :].bitcast(FP8)
+            if on == "S":
+                nc.scalar.activation(out=wide[u][:, j, :], in_=src, func=ACT.Copy, scale=scale)
+            else:
+                nc.vector.tensor_scalar(out=wide[u][:, j, :], in0=src, scalar1=scale, scalar2=None, op0=ALU.mult)
+
+        def weave(on, u):
+            woven[u] = ring("woven", u, 3, [P, SPAN * PACK], BF16)
+            if pieces[u][0] == 1:
+                dst = woven[u][:].rearrange("p (t m j) -> p t m j", t=PACK, j=PACK)
+                src = wide[u][:].rearrange("p j (m t) -> p t m j", t=PACK)
+            elif FAST:
+                dst = woven[u][:].rearrange("p (c i j) -> p c j i", i=4, j=PACK)
+                src = wide[u][:].rearrange("p j (c i) -> p c j i", i=4)
+            else:
+                dst = woven[u][:].rearrange("p (n j) -> p n j", j=PACK)
+                src = wide[u][:].rearrange("p j n -> p n j")
+            if on == "V":
+                nc.vector.tensor_copy(out=dst, in_=src)
+            elif on == "S":
+                nc.scalar.copy(out=dst, in_=src)
+            else:
+                nc.gpsimd.tensor_scalar(out=dst, in0=src, scalar1=1.0, scalar2=0.0, op0=ALU.mult, op1=ALU.add)
+
+        def quantize(name, src, words):
+            codes = keep.tile([P, words], U32, name=name + "_codes", align_bytes=64)
+            scales = keep.tile([P, words], U8, name=name + "_scales", align_bytes=64)
+            nc.vector.quantize_mx(out=codes[:].bitcast(FP8X4), scales=scales[:], in_=src)
+            return codes, scales
+
+        def quant_piece(on, u):
+            w_codes[pieces[u]], w_scales[pieces[u]] = quantize("w%d" % u, woven[u][:], SPAN)
+
+        def x_turn(on, i, pair):
+            words = x_sb[i][:].bitcast(F32)
+            bank = next_bank([P, 2, 2, P])
+            x_banks[i, pair] = bank
+            for k2 in range(2):
+                k = 2 * pair + k2
+                for u in range(2):
+                    nc.tensor.transpose(bank[:, k2, u, :], words[:, 256 * k + u : 256 * (k + 1) : 2], ident[:])
+
+        def x_copy(on, i, pair):
+            if i not in x_woven:
+                x_woven[i] = ring("xwoven", i, 2, [P, SPAN * PACK], BF16)
+            words = x_woven[i][:].bitcast(F32).rearrange("p (k r u) -> p k r u", k=4, u=2)
+            src = x_banks[i, pair][:].rearrange("p k u r -> p k r u")
+            if on == "S":
+                nc.scalar.copy(out=words[:, 2 * pair : 2 * pair + 2], in_=src)
+            else:
+                nc.vector.tensor_copy(out=words[:, 2 * pair : 2 * pair + 2], in_=src)
+
+        def x_quant(on, i):
+            x_codes[i], x_scales[i] = quantize("x%d" % i, x_woven[i][:], SPAN)
+
+        def mx(dst, lhs_c, lhs_s, rhs_c, rhs_s, start, stop):
+            nc.tensor.matmul_mx(out=dst, lhsT=lhs_c.bitcast(FP8X4), lhsT_scale=lhs_s, rhs=rhs_c.bitcast(FP8X4), rhs_scale=rhs_s, start=start, stop=stop)
+
+        def mm1(on, i, c):
+            bank = next_bank([P, PACK, P])
+            y_bank[i, c] = bank
+            for t in range(PACK):
+                ch = slice(t * P, (t + 1) * P)
+                for k in range(4):
+                    px = slice(k * P, (k + 1) * P)
+                    mx(bank[:, t, :], w_codes[1, k, c][:, ch], w_scales[1, k, c][:, ch], x_codes[i][:, px], x_scales[i][:, px], k == 0, k == 3)
+
+        def h_scale(on, i, c):
+            key = (i // 4, c)
+            if key not in h_woven:
+                h_woven[key] = ring("hwoven", 2 * key[0] + c, 4, [P, 4, P, PACK], BF16)
+            nc.vector.tensor_tensor(
+                out=h_woven[key][:, i % 4],
+                in0=y_bank[i, c][:].rearrange("p t r -> p r t"),
+                in1=g_sb[:, c, :].unsqueeze(1).to_broadcast([P, P, PACK]),
+                op=ALU.mult,
+            )
+
+        def h_quant(on, hf, c):
+            h_codes[hf, c], h_scales[hf, c] = quantize("h%d%d" % (hf, c), h_woven[hf, c][:].rearrange("p i r t -> p (i r t)"), SPAN)
+
+        def mm2(on, e, q):
+            c, hf = outs[e]
+            bank = next_bank([P, SPAN])
+            zt_bank[e, q] = bank
+            col = slice(q * P, (q + 1) * P)
+            for k in range(2):
+                if e in DIRECT:
+                    mx(bank[:], h_codes[hf, k][:, col], h_scales[hf, k][:, col], w_codes[2, k, c][:], w_scales[2, k, c][:], k == 0, k == 1)
+                else:
+                    mx(bank[:], w_codes[2, k, c][:, col], w_scales[2, k, c][:, col], h_codes[hf, k][:], h_scales[hf, k][:], k == 0, k == 1)
+
+        def add_bias(on, e, q):
+            c, hf = outs[e]
+            zt_sb[e, q] = ring("zt", 4 * e + q, 8, [P, SPAN], F32)
+            bias = b_col[:, 4 * c + q : 4 * c + q + 1]
+            if e in DIRECT:
+                nc.vector.tensor_tensor(out=zt_sb[e, q][:], in0=zt_bank[e, q][:], in1=b_wide[c][:], op=ALU.add)
+                z_src[e, q] = zt_sb[e, q]
+            elif on == "S":
+                nc.scalar.activation(out=zt_sb[e, q][:], in_=zt_bank[e, q][:], func=ACT.Identity, bias=bias)
+            else:
+                nc.vector.tensor_scalar(out=zt_sb[e, q][:], in0=zt_bank[e, q][:], scalar1=bias, scalar2=None, op0=ALU.add)
+
+        def turn_back(on, e, r):
+            bank = next_bank([P, SPAN])
+            z_src[e, r] = bank
+            for q in range(4):
+                nc.tensor.transpose(bank[:, q * P : (q + 1) * P], zt_sb[e, q][:, r * P : (r + 1) * P], ident[:])
+
+        def gate(on, e, r):
+            gate_sb[e, r] = ring("gate", 4 * e + r, 4, [P, SPAN], F32)
+            nc.scalar.activation(out=gate_sb[e, r][:], in_=z_src[e, r][:], func=ACT.Relu, bias=half[:], scale=1.0 / 6.0)
+
+        def finish(on, e, r):
+            res[e, r] = ring("res", 4 * e + r, 6, [P, SPAN], F32)
+            nc.vector.scalar_tensor_tensor(out=res[e, r][:], in0=gate_sb[e, r][:], scalar=1.0, in1=z_src[e, r][:], op0=ALU.min, op1=ALU.mult)
+
+        def store(on, e, r):
+            c, hf = outs[e]
+            i = 4 * hf + r
+            nc.sync.dma_start(out=out[i * P : (i + 1) * P, c * SPAN : (c + 1) * SPAN], in_=res[e, r][:])
+
+        outs = OUTS
+        res = {}
+        b_bank = {}
+
+        nc.sync.dma_start(out=s1[:], in_=W1_scale.rearrange("(k p j) o -> p k (j o)", p=P, j=PACK))
+        load_piece(0)
+        load_piece(1)
+        load_x(0)
+        load_piece(2)
+        load_piece(3)
+        load_x(1)
+        nc.sync.dma_start(out=g_sb[:], in_=g.rearrange("(k p j) -> p k j", p=P, j=PACK))
+        load_piece(4)
+        load_x(2)
+        load_piece(5)
+        load_x(3)
+        load_piece(6)
+        load_piece(7)
+        nc.sync.dma_start(out=s2[:], in_=W2_scale.rearrange("(k p j) o -> p k (j o)", p=P, j=PACK))
+        nc.sync.dma_start(out=b_rows[:], in_=b.rearrange("(q n) -> q n", n=P))
+        for i in range(4, 8):
+            load_x(i)
+        for u in range(8, 16):
+            load_piece(u)
+        for c in sorted(set(outs[e][0] for e in DIRECT)):
+            load_b_wide(c)
+
+        nc.vector.memset(half[:], 0.5)
+        make_identity(nc, ident[:])
+        nc.gpsimd.memset(b_sq[:], 0.0)
+        nc.scalar.activation(out=warm[:], in_=half[:], func=ACT.Relu, bias=half[:])
+
+        def b_copy(on):
+            nc.vector.tensor_copy(out=b_sq[: COUT // P, :], in_=b_rows[:])
+
+        def b_turn(on):
+            b_bank[0] = next_bank([P, P])
+            nc.tensor.transpose(b_bank[0][:], b_sq[:], ident[:])
+
+        def b_columns(on):
+            nc.scalar.copy(out=b_col[:], in_=b_bank[0][:, : COUT // P])
+
+        steps = {
+            "widen": widen, "weave": weave, "wq": quant_piece, "xturn": x_turn, "xcopy": x_copy, "xq": x_quant,
+            "mm1": mm1, "hs": h_scale, "hq": h_quant, "mm2": mm2, "bias": add_bias, "turn": turn_back, "gate": gate,
+            "fin": finish, "store": store, "bcopy": b_copy, "bturn": b_turn, "bcol": b_columns,
+        }
+        for entry in ORDER.split():
+            parts = entry.split(".")
+            steps[parts[0]](parts[1], *[int(a) for a in parts[2:]])

@@ -21,47 +21,47 @@ SPAN = P * PACK
 BANKS = 8
 
 DIRECT = ()
+WIDEU = ()
 OUTS = ((0, 0), (1, 0), (0, 1), (1, 1), (2, 0), (2, 1), (3, 0), (3, 1))
 ORDER = (
-    "widen.S.0.3 widen.V.0.2 widen.V.0.0 widen.S.0.1 widen.V.1.3 widen.S.1.1 widen.V.1.2 weave.V.0 widen.S.1.0 xturn.P.0.0 "
-    "weave.V.1 widen.S.2.2 xturn.P.0.1 xcopy.S.0.0 widen.S.2.3 widen.V.2.1 wq.V.0 xcopy.S.0.1 xturn.P.1.0 wq.V.1 "
-    "widen.S.2.0 xturn.P.1.1 xq.V.0 widen.S.3.2 xcopy.V.1.0 xcopy.S.1.1 widen.S.3.1 weave.V.2 widen.S.3.0 xturn.P.2.0 "
-    "xturn.P.2.1 widen.S.3.3 widen.V.4.1 widen.V.5.3 xcopy.S.2.0 wq.V.2 xcopy.S.2.1 weave.V.3 xturn.P.3.0 widen.S.5.1 "
-    "xturn.P.3.1 widen.S.5.2 xq.V.1 widen.S.6.0 widen.S.5.0 wq.V.3 widen.S.4.2 bcopy.V widen.V.6.3 mm1.P.0.0 "
-    "weave.V.5 widen.S.4.0 widen.S.4.3 xturn.P.4.1 widen.S.6.1 xq.V.2 xcopy.S.3.0 xturn.P.5.1 wq.V.5 xcopy.S.3.1 "
-    "xturn.P.4.0 weave.V.4 widen.S.7.3 xturn.P.6.0 widen.S.7.1 mm1.P.2.0 hs.V.0.0 widen.S.6.2 xq.V.3 xcopy.S.4.0 "
-    "xturn.P.5.0 weave.V.6 xcopy.S.4.1 mm1.P.1.0 widen.S.7.2 widen.S.9.0 wq.V.4 widen.S.7.0 mm1.P.3.0 xq.V.4 "
-    "xcopy.S.5.0 wq.V.6 widen.S.8.3 weave.V.7 bturn.P xcopy.S.5.1 xcopy.S.6.0 xturn.P.6.1 hs.V.2.0 widen.S.9.2 "
-    "xturn.P.7.1 wq.V.7 widen.S.9.1 xturn.P.7.0 hs.V.3.0 widen.S.9.3 mm1.P.1.1 xq.V.5 xcopy.S.6.1 hs.V.1.0 "
-    "widen.S.11.2 weave.V.9 mm1.P.2.1 widen.S.8.1 widen.S.8.0 widen.S.10.2 mm1.P.3.1 hq.V.0.0 widen.S.8.2 hs.V.2.1 "
-    "bcol.S widen.S.10.1 mm1.P.0.1 xq.V.6 xcopy.S.7.0 weave.V.8 widen.S.11.1 mm1.P.5.1 widen.S.10.0 hs.V.1.1 "
-    "xcopy.S.7.1 mm1.P.4.0 wq.V.8 widen.S.11.3 hs.V.0.1 widen.S.13.3 hs.V.3.1 mm1.P.6.0 widen.S.10.3 wq.V.9 "
-    "widen.S.13.2 hq.V.0.1 widen.S.12.3 mm1.P.4.1 xq.V.7 widen.S.13.1 weave.V.10 widen.S.11.0 mm2.P.0.3 mm2.P.0.2 "
-    "bias.S.0.3 mm2.P.0.1 hs.V.5.1 widen.S.12.1 mm2.P.0.0 hs.V.6.0 bias.S.0.1 mm1.P.6.1 hs.V.4.0 widen.S.14.0 "
-    "hs.V.4.1 widen.S.14.3 weave.V.11 mm1.P.7.0 bias.S.0.2 widen.S.13.0 mm1.P.5.0 hs.V.6.1 bias.S.0.0 wq.V.11 "
-    "widen.S.12.2 wq.V.10 mm1.P.7.1 widen.S.12.0 hs.V.5.0 widen.S.15.0 hs.V.7.0 widen.S.14.2 mm2.P.1.3 hs.V.7.1 "
-    "widen.S.14.1 mm2.P.1.1 weave.V.13 bias.S.1.3 mm2.P.1.2 mm2.P.1.0 bias.S.1.1 turn.P.0.3 hq.V.1.1 bias.S.1.2 "
-    "turn.P.0.0 hq.V.1.0 gate.S.0.3 turn.P.0.1 turn.P.0.2 widen.V.15.1 gate.S.0.0 mm2.P.2.3 weave.V.12 bias.S.1.0 "
-    "mm2.P.2.0 gate.S.0.1 mm2.P.2.1 fin.V.0.3 gate.S.0.2 turn.P.1.0 fin.V.0.0 store.D.0.3 bias.S.2.0 mm2.P.2.2 "
-    "widen.V.15.3 fin.V.0.1 gate.S.1.0 turn.P.1.3 fin.V.0.2 bias.S.2.3 mm2.P.3.2 store.D.0.1 store.D.0.0 fin.V.1.0 "
-    "bias.S.2.1 turn.P.1.1 bias.V.2.2 gate.S.1.3 store.D.1.0 turn.P.1.2 wq.V.12 mm2.P.3.3 gate.S.1.1 wq.V.13 "
-    "mm2.P.3.0 gate.S.1.2 fin.V.1.1 mm2.P.3.1 bias.S.3.2 fin.V.1.3 mm2.P.4.1 bias.S.3.0 widen.V.15.2 bias.S.3.3 "
-    "turn.P.2.0 store.D.1.3 fin.V.1.2 store.D.0.2 store.D.1.1 turn.P.2.1 weave.V.14 bias.S.3.1 turn.P.2.2 store.D.1.2 "
-    "turn.P.2.3 gate.S.2.0 mm2.P.4.0 gate.S.2.1 weave.V.15 mm2.P.4.3 bias.S.4.1 mm2.P.5.2 gate.S.2.2 mm2.P.4.2 "
-    "fin.V.2.0 gate.S.2.3 fin.V.2.1 bias.S.4.0 turn.P.3.1 fin.V.2.2 turn.P.3.0 store.D.2.1 bias.S.4.3 fin.V.2.3 "
-    "turn.P.3.2 gate.S.3.0 wq.V.15 turn.P.3.3 store.D.2.3 store.D.2.0 gate.S.3.1 store.D.2.2 bias.V.4.2 mm2.P.5.3 "
-    "bias.S.5.2 wq.V.14 mm2.P.5.0 gate.S.3.2 fin.V.3.1 turn.P.4.1 gate.S.3.3 fin.V.3.0 turn.P.4.3 store.D.3.1 "
-    "mm2.P.5.1 bias.S.5.3 fin.V.3.2 store.D.3.0 mm2.P.6.3 gate.S.4.1 fin.V.3.3 turn.P.4.2 bias.V.5.1 bias.S.5.0 "
-    "store.D.3.3 turn.P.4.0 fin.V.4.1 gate.S.4.3 mm2.P.6.1 bias.V.6.3 gate.S.4.2 mm2.P.6.0 fin.V.4.3 gate.S.4.0 "
-    "mm2.P.6.2 bias.V.6.1 bias.S.6.0 store.D.4.3 turn.P.5.1 store.D.4.1 store.D.3.2 fin.V.4.2 turn.P.5.3 gate.S.5.1 "
-    "turn.P.5.0 fin.V.4.0 store.D.4.2 mm2.P.7.0 gate.S.5.3 bias.V.6.2 store.D.4.0 turn.P.5.2 fin.V.5.1 gate.S.5.0 "
-    "turn.P.6.1 fin.V.5.3 gate.S.5.2 turn.P.6.3 store.D.5.1 mm2.P.7.2 fin.V.5.0 gate.S.6.1 mm2.P.7.1 bias.V.7.0 "
-    "gate.S.6.3 store.D.5.0 mm2.P.7.3 fin.V.6.1 bias.S.7.2 turn.P.6.0 fin.V.5.2 bias.S.7.1 store.D.6.1 store.D.5.3 "
-    "turn.P.6.2 bias.V.7.3 gate.S.6.0 store.D.5.2 fin.V.6.3 gate.S.6.2 turn.P.7.1 turn.P.7.3 fin.V.6.0 store.D.6.3 "
-    "gate.S.7.1 turn.P.7.0 fin.V.6.2 turn.P.7.2 gate.S.7.3 store.D.6.0 fin.V.7.1 store.D.6.2 gate.S.7.0 fin.V.7.3 "
-    "gate.S.7.2 store.D.7.1 fin.V.7.0 store.D.7.3 fin.V.7.2 store.D.7.0 store.D.7.2 "
+    "widen.S.0.2 widen.V.0.3 widen.V.0.1 widen.V.0.0 widen.S.1.0 widen.V.1.1 weave.V.0 widen.S.1.2 xturn.P.0.1 widen.S.1.3 "
+    "widen.V.2.0 widen.S.2.1 xturn.P.0.0 weave.V.1 widen.S.2.2 xturn.P.1.0 xcopy.S.0.1 wq.V.0 widen.S.2.3 xturn.P.1.1 "
+    "wq.V.1 widen.S.3.1 widen.V.3.2 xcopy.S.0.0 xturn.P.2.1 weave.V.2 xcopy.S.1.0 xturn.P.2.0 widen.S.3.3 xturn.P.3.1 "
+    "widen.V.3.0 xcopy.S.1.1 xturn.P.3.0 wq.V.2 xcopy.S.2.0 gcopy.V weave.V.3 xcopy.S.3.0 widen.S.4.1 xcopy.S.2.1 "
+    "xq.V.0.1 xcopy.S.3.1 xq.V.0.0 widen.S.5.2 wq.V.3 widen.S.4.3 bcopy.V widen.V.6.3 widen.S.6.1 xq.V.0.2 "
+    "widen.S.6.2 xturn.P.4.0 widen.V.4.0 xq.V.0.3 widen.S.4.2 widen.V.6.0 xturn.P.5.1 widen.S.5.0 widen.V.5.3 weave.V.4 "
+    "widen.S.5.1 xturn.P.4.1 xcopy.S.4.0 xcopy.S.5.1 weave.V.5 xturn.P.6.0 widen.S.7.3 xturn.P.5.0 widen.S.7.2 xturn.P.7.0 "
+    "wq.V.4 xturn.P.7.1 xcopy.S.6.0 weave.V.6 xturn.P.6.1 xcopy.S.5.0 mm1.P.0.0.1 xcopy.S.4.1 widen.V.7.1 widen.S.7.0 "
+    "wq.V.5 bturn.P xcopy.S.7.1 mm1.P.0.0.0 widen.V.8.1 xcopy.S.6.1 wq.V.6 xcopy.S.7.0 mm1.P.0.0.2 weave.V.7 "
+    "widen.S.9.3 mm1.P.0.0.3 hs.S.0.0.1 widen.V.9.0 hs.S.0.0.0 wq.V.7 widen.S.8.0 widen.V.8.3 mm1.P.0.1.2 xq.V.1.2 "
+    "widen.S.8.2 xq.V.1.3 mm1.P.0.1.0 xq.V.1.1 bcol.S hs.S.0.0.3 widen.V.10.3 mm1.P.0.1.1 hs.S.0.0.2 xq.V.1.0 "
+    "widen.S.9.1 mm1.P.0.1.3 weave.V.8 hs.S.0.1.1 mm1.P.1.1.2 hw.V.0.0 hs.S.0.1.0 mm1.P.1.0.0 widen.S.9.2 wq.V.8 "
+    "weave.V.10 mm1.P.1.0.2 hs.S.0.1.2 widen.S.10.2 mm1.P.1.0.3 weave.V.9 hs.S.0.1.3 mm1.P.1.0.1 hq.V.0.0 widen.S.10.0 "
+    "hw.V.0.1 mm1.P.1.1.3 hs.S.1.0.3 wq.V.9 widen.S.11.0 mm1.P.1.1.0 widen.V.11.2 hs.S.1.0.2 hq.V.0.1 hs.S.1.1.2 "
+    "weave.V.11 mm2.P.0.0 hs.S.1.0.0 mm2.P.0.3 hs.S.1.0.1 widen.V.10.1 mm2.P.0.2 hs.S.1.1.0 wq.V.10 mm1.P.1.1.1 "
+    "bias.S.0.3 hw.V.1.0 bias.S.0.0 mm2.P.0.1 hs.S.1.1.3 wq.V.11 bias.S.0.2 weave.V.12 mm2.P.1.1 hs.S.1.1.1 "
+    "mm2.P.1.2 bias.S.0.1 hq.V.1.0 mm2.P.1.3 bias.S.1.1 hw.V.1.1 turn.P.0.1 bias.S.1.2 turn.P.0.3 turn.P.0.2 "
+    "gate.S.0.1 widen.V.11.1 mm2.P.1.0 bias.S.1.3 hq.V.1.1 turn.P.0.0 gate.S.0.3 widen.V.11.3 mm2.P.2.0 gate.S.0.2 "
+    "fin.V.0.1 mm2.P.2.3 wq.V.12 gate.S.0.0 store.D.0.1 mm2.P.2.2 fin.V.0.3 bias.S.1.0 mm2.P.2.1 fin.V.0.2 "
+    "bias.S.2.0 store.D.0.3 turn.P.1.0 fin.V.0.0 bias.S.2.3 store.D.0.2 turn.P.1.3 bias.V.2.2 turn.P.1.1 bias.S.2.1 "
+    "store.D.0.0 turn.P.1.2 weave.V.13 mm2.P.3.1 gate.S.1.0 mm2.P.3.0 gate.S.1.1 fin.V.1.0 mm2.P.3.2 gate.S.1.3 "
+    "fin.V.1.1 mm2.P.3.3 gate.S.1.2 store.D.1.0 turn.P.2.1 fin.V.1.3 bias.S.3.2 fin.V.1.2 bias.S.3.0 turn.P.2.0 "
+    "wq.V.13 turn.P.2.2 store.D.1.2 bias.S.3.1 turn.P.2.3 store.D.1.1 store.D.1.3 bias.V.3.3 gate.S.2.1 weave.V.14 "
+    "mm2.P.4.0 gate.S.2.0 mm2.P.4.2 gate.S.2.2 mm2.P.4.3 fin.V.2.1 gate.S.2.3 mm2.P.4.1 fin.V.2.0 store.D.2.1 "
+    "bias.S.4.3 turn.P.3.1 fin.V.2.2 store.D.2.0 mm2.P.5.0 bias.S.4.0 fin.V.2.3 store.D.2.2 gate.S.3.1 mm2.P.5.2 "
+    "weave.V.15 store.D.2.3 turn.P.3.0 bias.S.4.2 turn.P.3.2 bias.S.4.1 fin.V.3.1 turn.P.3.3 gate.S.3.0 mm2.P.5.3 "
+    "wq.V.14 gate.S.3.2 mm2.P.5.1 bias.V.5.2 turn.P.4.1 bias.S.5.0 fin.V.3.0 gate.S.3.3 fin.V.3.2 turn.P.4.0 "
+    "store.D.3.0 store.D.3.1 bias.S.5.3 turn.P.4.3 wq.V.15 turn.P.4.2 gate.S.4.1 fin.V.3.3 mm2.P.6.1 bias.V.5.1 "
+    "gate.S.4.0 store.D.3.3 mm2.P.6.2 store.D.3.2 fin.V.4.1 gate.S.4.3 mm2.P.6.0 fin.V.4.0 gate.S.4.2 mm2.P.6.3 "
+    "fin.V.4.3 bias.S.6.1 turn.P.5.1 store.D.4.0 store.D.4.1 fin.V.4.2 turn.P.5.0 bias.S.6.2 turn.P.5.3 bias.V.6.3 "
+    "gate.S.5.1 store.D.4.2 turn.P.5.2 store.D.4.3 bias.V.6.0 mm2.P.7.3 gate.S.5.0 fin.V.5.1 mm2.P.7.0 gate.S.5.3 "
+    "fin.V.5.0 turn.P.6.1 bias.S.7.3 turn.P.6.0 fin.V.5.3 mm2.P.7.2 store.D.5.0 gate.S.5.2 bias.V.7.0 store.D.5.3 "
+    "mm2.P.7.1 gate.S.6.1 store.D.5.1 fin.V.5.2 turn.P.6.2 gate.S.6.0 fin.V.6.1 store.D.5.2 turn.P.6.3 bias.S.7.2 "
+    "bias.V.7.1 store.D.6.1 gate.S.6.2 fin.V.6.0 turn.P.7.0 gate.S.6.3 turn.P.7.1 fin.V.6.2 store.D.6.0 turn.P.7.3 "
+    "gate.S.7.0 turn.P.7.2 fin.V.6.3 store.D.6.2 gate.S.7.1 fin.V.7.0 store.D.6.3 gate.S.7.3 fin.V.7.1 store.D.7.0 "
+    "gate.S.7.2 fin.V.7.3 store.D.7.1 fin.V.7.2 store.D.7.3 store.D.7.2 "
 )
-FAST = False
+FAST = True
 
 
 def tile_pointwise_bottleneck_hardswish_d5_kernel(tc, x, W1_bytes, W1_scale, g, W2_bytes, W2_scale, b, out):
@@ -85,6 +85,7 @@ def tile_pointwise_bottleneck_hardswish_d5_kernel(tc, x, W1_bytes, W1_scale, g, 
         s1 = keep.tile([P, CIN // SPAN, PACK], F32, name="s1")
         s2 = keep.tile([P, MID // SPAN, PACK], F32, name="s2")
         g_sb = keep.tile([P, MID // SPAN, PACK], BF16, name="g_sb")
+        g_col = keep.tile([P, MID // SPAN, PACK], F32, name="g_col")
         b_rows = keep.tile([COUT // P, P], BF16, name="b_rows")
         b_sq = keep.tile([P, P], F32, name="b_sq")
         b_col = keep.tile([P, COUT // P], F32, name="b_col")
@@ -97,17 +98,19 @@ def tile_pointwise_bottleneck_hardswish_d5_kernel(tc, x, W1_bytes, W1_scale, g, 
         y_bank, h_woven, h_codes, h_scales = {}, {}, {}, {}
         zt_bank, zt_sb, z_src, gate_sb, b_wide = {}, {}, {}, {}, {}
 
-        def load_piece(u):
-            which, k, c = pieces[u]
-            src = W1_bytes if which == 1 else W2_bytes
-            raw[u] = keep.tile([P, PACK, SPAN], U8, name="raw%d" % u, align_bytes=64)
-            nc.sync.dma_start(
-                out=raw[u][:],
-                in_=src[k * SPAN : (k + 1) * SPAN, c * SPAN : (c + 1) * SPAN].rearrange("(p j) n -> p j n", j=PACK),
-            )
+        def load_of(u):
+            return u if u < 8 else 8 + 2 * ((u - 8) // 4) + u % 2
+
+        def load_piece(l):
+            if l < 8:
+                src, k, cols = W1_bytes, l % 4, slice(l // 4 * SPAN, (l // 4 + 1) * SPAN)
+            else:
+                src, k, cols = W2_bytes, l % 2, slice((l - 8) // 2 * 2 * SPAN, ((l - 8) // 2 + 1) * 2 * SPAN)
+            raw[l] = keep.tile([P, PACK, cols.stop - cols.start], U8, name="raw%d" % l, align_bytes=64)
+            nc.sync.dma_start(out=raw[l][:], in_=src[k * SPAN : (k + 1) * SPAN, cols].rearrange("(p j) n -> p j n", j=PACK))
 
         def load_x(i):
-            x_sb[i] = keep.tile([P, CIN], BF16, name="x%d" % i, align_bytes=64)
+            x_sb[i] = keep.tile([P, CIN], BF16, name="slot%d" % i, align_bytes=64)
             nc.sync.dma_start(out=x_sb[i][:], in_=x[i * P : (i + 1) * P, :])
 
         def load_b_wide(c):
@@ -115,33 +118,39 @@ def tile_pointwise_bottleneck_hardswish_d5_kernel(tc, x, W1_bytes, W1_scale, g, 
             nc.sync.dma_start(out=b_wide[c][:], in_=b[c * SPAN : (c + 1) * SPAN].partition_broadcast(P))
 
         def widen(on, u, j):
-            which, k, c = pieces[u]
-            scale = (s1 if which == 1 else s2)[:, k, j : j + 1]
+            scale = s1[:, u % 4, j : j + 1] if u < 8 else s2[:, u % 2, j : j + 1]
             if u not in wide:
-                wide[u] = ring("wide", u, 4, [P, PACK, SPAN], BF16)
+                if u < 8:
+                    wide[u] = ring("wide1_", u, 3, [P, PACK, SPAN], BF16)
+                else:
+                    wide[u] = ring("wide2_", u - 8, 3, [P, PACK, 2 * SPAN], BF16)
             src = raw[u][:, j, :].bitcast(FP8)
             if on == "S":
                 nc.scalar.activation(out=wide[u][:, j, :], in_=src, func=ACT.Copy, scale=scale)
             else:
                 nc.vector.tensor_scalar(out=wide[u][:, j, :], in0=src, scalar1=scale, scalar2=None, op0=ALU.mult)
 
+        def interleave(on, dst, src):
+            if on == "V" and FAST:
+                nc.vector.tensor_copy(out=dst.rearrange("p (c i j) -> p c j i", i=4, j=PACK), in_=src.rearrange("p j (c i) -> p c j i", i=4))
+            elif on == "V":
+                nc.vector.tensor_copy(out=dst.rearrange("p (n j) -> p n j", j=PACK), in_=src.rearrange("p j n -> p n j"))
+            else:
+                nc.gpsimd.tensor_scalar(
+                    out=dst.rearrange("p (n j) -> p n j", j=PACK), in0=src.rearrange("p j n -> p n j"),
+                    scalar1=1.0, scalar2=0.0, op0=ALU.mult, op1=ALU.add,
+                )
+
         def weave(on, u):
             woven[u] = ring("woven", u, 3, [P, SPAN * PACK], BF16)
-            if pieces[u][0] == 1:
-                dst = woven[u][:].rearrange("p (t m j) -> p t m j", t=PACK, j=PACK)
-                src = wide[u][:].rearrange("p j (m t) -> p t m j", t=PACK)
-            elif FAST:
-                dst = woven[u][:].rearrange("p (c i j) -> p c j i", i=4, j=PACK)
-                src = wide[u][:].rearrange("p j (c i) -> p c j i", i=4)
+            if u < 8:
+                nc.vector.tensor_copy(
+                    out=woven[u][:].rearrange("p (t a m j) -> p a t m j", t=PACK, m=2, j=PACK),
+                    in_=wide[u][:].rearrange("p j (a m t) -> p a t m j", m=2, t=PACK),
+                )
             else:
-                dst = woven[u][:].rearrange("p (n j) -> p n j", j=PACK)
-                src = wide[u][:].rearrange("p j n -> p n j")
-            if on == "V":
-                nc.vector.tensor_copy(out=dst, in_=src)
-            elif on == "S":
-                nc.scalar.copy(out=dst, in_=src)
-            else:
-                nc.gpsimd.tensor_scalar(out=dst, in0=src, scalar1=1.0, scalar2=0.0, op0=ALU.mult, op1=ALU.add)
+                side = pieces[u][2] % 2
+                interleave(on, woven[u][:], wide[load_of(u)][:, :, side * SPAN : (side + 1) * SPAN])
 
         def quantize(name, src, words):
             codes = keep.tile([P, words], U32, name=name + "_codes", align_bytes=64)
@@ -162,43 +171,54 @@ def tile_pointwise_bottleneck_hardswish_d5_kernel(tc, x, W1_bytes, W1_scale, g, 
                     nc.tensor.transpose(bank[:, k2, u, :], words[:, 256 * k + u : 256 * (k + 1) : 2], ident[:])
 
         def x_copy(on, i, pair):
-            if i not in x_woven:
-                x_woven[i] = ring("xwoven", i, 2, [P, SPAN * PACK], BF16)
-            words = x_woven[i][:].bitcast(F32).rearrange("p (k r u) -> p k r u", k=4, u=2)
+            key = (i // 4, pair)
+            if key not in x_woven:
+                x_woven[key] = ring("xwoven", pair, 2, [P, 2, SPAN * PACK], BF16)
+            words = x_woven[key][:].bitcast(F32).rearrange("p k (i r u) -> p k i r u", i=4, u=2)[:, :, i % 4]
             src = x_banks[i, pair][:].rearrange("p k u r -> p k r u")
             if on == "S":
-                nc.scalar.copy(out=words[:, 2 * pair : 2 * pair + 2], in_=src)
+                nc.scalar.copy(out=words, in_=src)
             else:
-                nc.vector.tensor_copy(out=words[:, 2 * pair : 2 * pair + 2], in_=src)
+                nc.vector.tensor_copy(out=words, in_=src)
 
-        def x_quant(on, i):
-            x_codes[i], x_scales[i] = quantize("x%d" % i, x_woven[i][:], SPAN)
+        def x_quant(on, hf, k):
+            x_codes[hf, k], x_scales[hf, k] = quantize("x%d%d" % (hf, k), x_woven[hf, k // 2][:, k % 2, :], SPAN)
 
         def mx(dst, lhs_c, lhs_s, rhs_c, rhs_s, start, stop):
             nc.tensor.matmul_mx(out=dst, lhsT=lhs_c.bitcast(FP8X4), lhsT_scale=lhs_s, rhs=rhs_c.bitcast(FP8X4), rhs_scale=rhs_s, start=start, stop=stop)
 
-        def mm1(on, i, c):
-            bank = next_bank([P, PACK, P])
-            y_bank[i, c] = bank
-            for t in range(PACK):
-                ch = slice(t * P, (t + 1) * P)
-                for k in range(4):
-                    px = slice(k * P, (k + 1) * P)
-                    mx(bank[:, t, :], w_codes[1, k, c][:, ch], w_scales[1, k, c][:, ch], x_codes[i][:, px], x_scales[i][:, px], k == 0, k == 3)
+        def mm1(on, hf, c, t):
+            bank = next_bank([P, SPAN])
+            y_bank[hf, c, t] = bank
+            ch = slice(t * P, (t + 1) * P)
+            for k in range(4):
+                mx(bank[:], w_codes[1, k, c][:, ch], w_scales[1, k, c][:, ch], x_codes[hf, k][:], x_scales[hf, k][:], k == 0, k == 3)
 
-        def h_scale(on, i, c):
-            key = (i // 4, c)
-            if key not in h_woven:
-                h_woven[key] = ring("hwoven", 2 * key[0] + c, 4, [P, 4, P, PACK], BF16)
-            nc.vector.tensor_tensor(
-                out=h_woven[key][:, i % 4],
-                in0=y_bank[i, c][:].rearrange("p t r -> p r t"),
-                in1=g_sb[:, c, :].unsqueeze(1).to_broadcast([P, P, PACK]),
-                op=ALU.mult,
-            )
+        def h_scale(on, hf, c, t):
+            if (hf, c) not in h_rows:
+                h_rows[hf, c] = ring("hrows", c, 2, [P, PACK, SPAN], BF16)
+            if on == "S":
+                nc.scalar.activation(out=h_rows[hf, c][:, t, :], in_=y_bank[hf, c, t][:], func=ACT.Copy, scale=g_col[:, c, t : t + 1])
+            else:
+                nc.vector.tensor_scalar(out=h_rows[hf, c][:, t, :], in0=y_bank[hf, c, t][:], scalar1=g_col[:, c, t : t + 1], scalar2=None, op0=ALU.mult)
+
+        def h_weave(on, hf, c):
+            h_woven[hf, c] = ring("hwoven", c, 2, [P, SPAN * PACK], BF16)
+            interleave(on, h_woven[hf, c][:], h_rows[hf, c][:])
 
         def h_quant(on, hf, c):
-            h_codes[hf, c], h_scales[hf, c] = quantize("h%d%d" % (hf, c), h_woven[hf, c][:].rearrange("p i r t -> p (i r t)"), SPAN)
+            h_codes[hf, c], h_scales[hf, c] = quantize("h%d%d" % (hf, c), h_woven[hf, c][:], SPAN)
+
+        def g_copy(on):
+            nc.vector.tensor_copy(out=g_col[:], in_=g_sb[:])
+
+        pairs = {}
+
+        def pair_tile(kind, first, depth, e, q):
+            n = 2 * e + q // 2
+            if (kind, n) not in pairs:
+                pairs[kind, n] = keep.tile([P, 2, SPAN], F32, name="slot%d" % (first + n % depth), align_bytes=64)
+            return pairs[kind, n]
 
         def mm2(on, e, q):
             c, hf = outs[e]
@@ -213,58 +233,64 @@ def tile_pointwise_bottleneck_hardswish_d5_kernel(tc, x, W1_bytes, W1_scale, g, 
 
         def add_bias(on, e, q):
             c, hf = outs[e]
-            zt_sb[e, q] = ring("zt", 4 * e + q, 8, [P, SPAN], F32)
+            zt_sb[e, q] = pair_tile("zt", 0, 4, e, q)[:, q % 2, :]
             bias = b_col[:, 4 * c + q : 4 * c + q + 1]
             if e in DIRECT:
-                nc.vector.tensor_tensor(out=zt_sb[e, q][:], in0=zt_bank[e, q][:], in1=b_wide[c][:], op=ALU.add)
-                z_src[e, q] = zt_sb[e, q]
+                nc.vector.tensor_tensor(out=zt_sb[e, q], in0=zt_bank[e, q][:], in1=b_wide[c][:], op=ALU.add)
             elif on == "S":
-                nc.scalar.activation(out=zt_sb[e, q][:], in_=zt_bank[e, q][:], func=ACT.Identity, bias=bias)
+                nc.scalar.activation(out=zt_sb[e, q], in_=zt_bank[e, q][:], func=ACT.Identity, bias=bias)
             else:
-                nc.vector.tensor_scalar(out=zt_sb[e, q][:], in0=zt_bank[e, q][:], scalar1=bias, scalar2=None, op0=ALU.add)
+                nc.vector.tensor_scalar(out=zt_sb[e, q], in0=zt_bank[e, q][:], scalar1=bias, scalar2=None, op0=ALU.add)
 
         def turn_back(on, e, r):
             bank = next_bank([P, SPAN])
-            z_src[e, r] = bank
+            z_src[e, r] = bank[:]
             for q in range(4):
                 nc.tensor.transpose(bank[:, q * P : (q + 1) * P], zt_sb[e, q][:, r * P : (r + 1) * P], ident[:])
 
+        def part(kind, first, depth, e, r):
+            tile = pair_tile(kind, first, depth, e, r)
+            return tile[:].rearrange("p a n -> p (a n)") if e in WIDEU else tile[:, r % 2, :]
+
+        def z_of(e, r):
+            return part("zt", 0, 4, e, r) if e in DIRECT else z_src[e, r]
+
         def gate(on, e, r):
-            gate_sb[e, r] = ring("gate", 4 * e + r, 4, [P, SPAN], F32)
-            nc.scalar.activation(out=gate_sb[e, r][:], in_=z_src[e, r][:], func=ACT.Relu, bias=half[:], scale=1.0 / 6.0)
+            nc.scalar.activation(out=part("gate", 4, 2, e, r), in_=z_of(e, r), func=ACT.Relu, bias=half[:], scale=1.0 / 6.0)
 
         def finish(on, e, r):
-            res[e, r] = ring("res", 4 * e + r, 6, [P, SPAN], F32)
-            nc.vector.scalar_tensor_tensor(out=res[e, r][:], in0=gate_sb[e, r][:], scalar=1.0, in1=z_src[e, r][:], op0=ALU.min, op1=ALU.mult)
+            nc.vector.scalar_tensor_tensor(out=part("res", 6, 3, e, r), in0=part("gate", 4, 2, e, r), scalar=1.0, in1=z_of(e, r), op0=ALU.min, op1=ALU.mult)
 
         def store(on, e, r):
             c, hf = outs[e]
             i = 4 * hf + r
-            nc.sync.dma_start(out=out[i * P : (i + 1) * P, c * SPAN : (c + 1) * SPAN], in_=res[e, r][:])
+            cols = slice(c * SPAN, (c + 1) * SPAN)
+            if e in WIDEU:
+                nc.sync.dma_start(out=out[i * P : (i + 2) * P, cols].rearrange("(a p) n -> p a n", p=P), in_=pair_tile("res", 6, 3, e, r)[:])
+            else:
+                nc.sync.dma_start(out=out[i * P : (i + 1) * P, cols], in_=part("res", 6, 3, e, r))
 
         outs = OUTS
-        res = {}
+        h_rows = {}
         b_bank = {}
 
-        nc.sync.dma_start(out=s1[:], in_=W1_scale.rearrange("(k p j) o -> p k (j o)", p=P, j=PACK))
+        nc.scalar.dma_start(out=s1[:], in_=W1_scale.rearrange("(k p j) o -> p k (j o)", p=P, j=PACK))
         load_piece(0)
         load_piece(1)
         load_x(0)
         load_piece(2)
-        load_piece(3)
         load_x(1)
-        nc.sync.dma_start(out=g_sb[:], in_=g.rearrange("(k p j) -> p k j", p=P, j=PACK))
-        load_piece(4)
+        load_piece(3)
         load_x(2)
-        load_piece(5)
         load_x(3)
-        load_piece(6)
-        load_piece(7)
+        nc.sync.dma_start(out=g_sb[:], in_=g.rearrange("(k p j) -> p k j", p=P, j=PACK))
+        for u in range(4, 8):
+            load_piece(u)
         nc.sync.dma_start(out=s2[:], in_=W2_scale.rearrange("(k p j) o -> p k (j o)", p=P, j=PACK))
         nc.sync.dma_start(out=b_rows[:], in_=b.rearrange("(q n) -> q n", n=P))
         for i in range(4, 8):
             load_x(i)
-        for u in range(8, 16):
+        for u in range(8, 12):
             load_piece(u)
         for c in sorted(set(outs[e][0] for e in DIRECT)):
             load_b_wide(c)
@@ -286,7 +312,7 @@ def tile_pointwise_bottleneck_hardswish_d5_kernel(tc, x, W1_bytes, W1_scale, g, 
 
         steps = {
             "widen": widen, "weave": weave, "wq": quant_piece, "xturn": x_turn, "xcopy": x_copy, "xq": x_quant,
-            "mm1": mm1, "hs": h_scale, "hq": h_quant, "mm2": mm2, "bias": add_bias, "turn": turn_back, "gate": gate,
+            "mm1": mm1, "hs": h_scale, "hw": h_weave, "hq": h_quant, "gcopy": g_copy, "mm2": mm2, "bias": add_bias, "turn": turn_back, "gate": gate,
             "fin": finish, "store": store, "bcopy": b_copy, "bturn": b_turn, "bcol": b_columns,
         }
         for entry in ORDER.split():

@@ -23,44 +23,9 @@ BANKS = 8
 DIRECT = ()
 WIDEU = ()
 OUTS = ((0, 0), (1, 0), (0, 1), (1, 1), (2, 0), (2, 1), (3, 0), (3, 1))
-ORDER = (
-    "widen.S.0.2 widen.V.0.3 widen.V.0.1 widen.V.0.0 widen.S.1.0 widen.V.1.1 weave.V.0 widen.S.1.2 xturn.P.0.1 widen.S.1.3 "
-    "widen.V.2.0 widen.S.2.1 xturn.P.0.0 weave.V.1 widen.S.2.2 xturn.P.1.0 xcopy.S.0.1 wq.V.0 widen.S.2.3 xturn.P.1.1 "
-    "wq.V.1 widen.S.3.1 widen.V.3.2 xcopy.S.0.0 xturn.P.2.1 weave.V.2 xcopy.S.1.0 xturn.P.2.0 widen.S.3.3 xturn.P.3.1 "
-    "widen.V.3.0 xcopy.S.1.1 xturn.P.3.0 wq.V.2 xcopy.S.2.0 gcopy.V weave.V.3 xcopy.S.3.0 widen.S.4.1 xcopy.S.2.1 "
-    "xq.V.0.1 xcopy.S.3.1 xq.V.0.0 widen.S.5.2 wq.V.3 widen.S.4.3 bcopy.V widen.V.6.3 widen.S.6.1 xq.V.0.2 "
-    "widen.S.6.2 xturn.P.4.0 widen.V.4.0 xq.V.0.3 widen.S.4.2 widen.V.6.0 xturn.P.5.1 widen.S.5.0 widen.V.5.3 weave.V.4 "
-    "widen.S.5.1 xturn.P.4.1 xcopy.S.4.0 xcopy.S.5.1 weave.V.5 xturn.P.6.0 widen.S.7.3 xturn.P.5.0 widen.S.7.2 xturn.P.7.0 "
-    "wq.V.4 xturn.P.7.1 xcopy.S.6.0 weave.V.6 xturn.P.6.1 xcopy.S.5.0 mm1.P.0.0.1 xcopy.S.4.1 widen.V.7.1 widen.S.7.0 "
-    "wq.V.5 bturn.P xcopy.S.7.1 mm1.P.0.0.0 widen.V.8.1 xcopy.S.6.1 wq.V.6 xcopy.S.7.0 mm1.P.0.0.2 weave.V.7 "
-    "widen.S.9.3 mm1.P.0.0.3 hs.S.0.0.1 widen.V.9.0 hs.S.0.0.0 wq.V.7 widen.S.8.0 widen.V.8.3 mm1.P.0.1.2 xq.V.1.2 "
-    "widen.S.8.2 xq.V.1.3 mm1.P.0.1.0 xq.V.1.1 bcol.S hs.S.0.0.3 widen.V.10.3 mm1.P.0.1.1 hs.S.0.0.2 xq.V.1.0 "
-    "widen.S.9.1 mm1.P.0.1.3 weave.V.8 hs.S.0.1.1 mm1.P.1.1.2 hw.V.0.0 hs.S.0.1.0 mm1.P.1.0.0 widen.S.9.2 wq.V.8 "
-    "weave.V.10 mm1.P.1.0.2 hs.S.0.1.2 widen.S.10.2 mm1.P.1.0.3 weave.V.9 hs.S.0.1.3 mm1.P.1.0.1 hq.V.0.0 widen.S.10.0 "
-    "hw.V.0.1 mm1.P.1.1.3 hs.S.1.0.3 wq.V.9 widen.S.11.0 mm1.P.1.1.0 widen.V.11.2 hs.S.1.0.2 hq.V.0.1 hs.S.1.1.2 "
-    "weave.V.11 mm2.P.0.0 hs.S.1.0.0 mm2.P.0.3 hs.S.1.0.1 widen.V.10.1 mm2.P.0.2 hs.S.1.1.0 wq.V.10 mm1.P.1.1.1 "
-    "bias.S.0.3 hw.V.1.0 bias.S.0.0 mm2.P.0.1 hs.S.1.1.3 wq.V.11 bias.S.0.2 weave.V.12 mm2.P.1.1 hs.S.1.1.1 "
-    "mm2.P.1.2 bias.S.0.1 hq.V.1.0 mm2.P.1.3 bias.S.1.1 hw.V.1.1 turn.P.0.1 bias.S.1.2 turn.P.0.3 turn.P.0.2 "
-    "gate.S.0.1 widen.V.11.1 mm2.P.1.0 bias.S.1.3 hq.V.1.1 turn.P.0.0 gate.S.0.3 widen.V.11.3 mm2.P.2.0 gate.S.0.2 "
-    "fin.V.0.1 mm2.P.2.3 wq.V.12 gate.S.0.0 store.D.0.1 mm2.P.2.2 fin.V.0.3 bias.S.1.0 mm2.P.2.1 fin.V.0.2 "
-    "bias.S.2.0 store.D.0.3 turn.P.1.0 fin.V.0.0 bias.S.2.3 store.D.0.2 turn.P.1.3 bias.V.2.2 turn.P.1.1 bias.S.2.1 "
-    "store.D.0.0 turn.P.1.2 weave.V.13 mm2.P.3.1 gate.S.1.0 mm2.P.3.0 gate.S.1.1 fin.V.1.0 mm2.P.3.2 gate.S.1.3 "
-    "fin.V.1.1 mm2.P.3.3 gate.S.1.2 store.D.1.0 turn.P.2.1 fin.V.1.3 bias.S.3.2 fin.V.1.2 bias.S.3.0 turn.P.2.0 "
-    "wq.V.13 turn.P.2.2 store.D.1.2 bias.S.3.1 turn.P.2.3 store.D.1.1 store.D.1.3 bias.V.3.3 gate.S.2.1 weave.V.14 "
-    "mm2.P.4.0 gate.S.2.0 mm2.P.4.2 gate.S.2.2 mm2.P.4.3 fin.V.2.1 gate.S.2.3 mm2.P.4.1 fin.V.2.0 store.D.2.1 "
-    "bias.S.4.3 turn.P.3.1 fin.V.2.2 store.D.2.0 mm2.P.5.0 bias.S.4.0 fin.V.2.3 store.D.2.2 gate.S.3.1 mm2.P.5.2 "
-    "weave.V.15 store.D.2.3 turn.P.3.0 bias.S.4.2 turn.P.3.2 bias.S.4.1 fin.V.3.1 turn.P.3.3 gate.S.3.0 mm2.P.5.3 "
-    "wq.V.14 gate.S.3.2 mm2.P.5.1 bias.V.5.2 turn.P.4.1 bias.S.5.0 fin.V.3.0 gate.S.3.3 fin.V.3.2 turn.P.4.0 "
-    "store.D.3.0 store.D.3.1 bias.S.5.3 turn.P.4.3 wq.V.15 turn.P.4.2 gate.S.4.1 fin.V.3.3 mm2.P.6.1 bias.V.5.1 "
-    "gate.S.4.0 store.D.3.3 mm2.P.6.2 store.D.3.2 fin.V.4.1 gate.S.4.3 mm2.P.6.0 fin.V.4.0 gate.S.4.2 mm2.P.6.3 "
-    "fin.V.4.3 bias.S.6.1 turn.P.5.1 store.D.4.0 store.D.4.1 fin.V.4.2 turn.P.5.0 bias.S.6.2 turn.P.5.3 bias.V.6.3 "
-    "gate.S.5.1 store.D.4.2 turn.P.5.2 store.D.4.3 bias.V.6.0 mm2.P.7.3 gate.S.5.0 fin.V.5.1 mm2.P.7.0 gate.S.5.3 "
-    "fin.V.5.0 turn.P.6.1 bias.S.7.3 turn.P.6.0 fin.V.5.3 mm2.P.7.2 store.D.5.0 gate.S.5.2 bias.V.7.0 store.D.5.3 "
-    "mm2.P.7.1 gate.S.6.1 store.D.5.1 fin.V.5.2 turn.P.6.2 gate.S.6.0 fin.V.6.1 store.D.5.2 turn.P.6.3 bias.S.7.2 "
-    "bias.V.7.1 store.D.6.1 gate.S.6.2 fin.V.6.0 turn.P.7.0 gate.S.6.3 turn.P.7.1 fin.V.6.2 store.D.6.0 turn.P.7.3 "
-    "gate.S.7.0 turn.P.7.2 fin.V.6.3 store.D.6.2 gate.S.7.1 fin.V.7.0 store.D.6.3 gate.S.7.3 fin.V.7.1 store.D.7.0 "
-    "gate.S.7.2 fin.V.7.3 store.D.7.1 fin.V.7.2 store.D.7.3 store.D.7.2 "
-)
+V_ROWS = [2,2,1,1,1,2,2,2]
+V_BIAS = [0, 2, 2, 1, 2, 2, 2, 2]
+QAT = [3, 3]
 FAST = True
 
 
@@ -82,7 +47,8 @@ def tile_pointwise_bottleneck_hardswish_d5_kernel(tc, x, W1_bytes, W1_scale, g, 
             return keep.tile(shape, dtype, name="%s%d" % (kind, n % depth), align_bytes=64)
 
         ident = keep.tile([P, P], F32, name="ident")
-        s1 = keep.tile([P, CIN // SPAN, PACK], F32, name="s1")
+        s0 = keep.tile([P, 1, PACK], F32, name="s0")
+        s1 = keep.tile([P, CIN // SPAN - 1, PACK], F32, name="s1")
         s2 = keep.tile([P, MID // SPAN, PACK], F32, name="s2")
         g_sb = keep.tile([P, MID // SPAN, PACK], BF16, name="g_sb")
         g_col = keep.tile([P, MID // SPAN, PACK], F32, name="g_col")
@@ -99,15 +65,21 @@ def tile_pointwise_bottleneck_hardswish_d5_kernel(tc, x, W1_bytes, W1_scale, g, 
         zt_bank, zt_sb, z_src, gate_sb, b_wide = {}, {}, {}, {}, {}
 
         def load_of(u):
-            return u if u < 8 else 8 + 2 * ((u - 8) // 4) + u % 2
+            return u % 4 if u < 8 else 4 + 2 * ((u - 8) // 4) + u % 2
 
         def load_piece(l):
-            if l < 8:
-                src, k, cols = W1_bytes, l % 4, slice(l // 4 * SPAN, (l // 4 + 1) * SPAN)
+            if l < 4:
+                src = W1_bytes[l * SPAN : (l + 1) * SPAN, :]
             else:
-                src, k, cols = W2_bytes, l % 2, slice((l - 8) // 2 * 2 * SPAN, ((l - 8) // 2 + 1) * 2 * SPAN)
-            raw[l] = keep.tile([P, PACK, cols.stop - cols.start], U8, name="raw%d" % l, align_bytes=64)
-            nc.sync.dma_start(out=raw[l][:], in_=src[k * SPAN : (k + 1) * SPAN, cols].rearrange("(p j) n -> p j n", j=PACK))
+                k, pair = l % 2, (l - 4) // 2
+                src = W2_bytes[k * SPAN : (k + 1) * SPAN, pair * 2 * SPAN : (pair + 1) * 2 * SPAN]
+            src = src.rearrange("(p j) n -> p j n", j=PACK)
+            raw[l] = keep.tile([P, PACK, 2 * SPAN], U8, name="raw%d" % l, align_bytes=64)
+            if l == 0:
+                for j in range(PACK):
+                    nc.sync.dma_start(out=raw[l][:, j, :], in_=src[:, j, :])
+            else:
+                nc.sync.dma_start(out=raw[l][:], in_=src)
 
         def load_x(i):
             x_sb[i] = keep.tile([P, CIN], BF16, name="slot%d" % i, align_bytes=64)
@@ -118,12 +90,9 @@ def tile_pointwise_bottleneck_hardswish_d5_kernel(tc, x, W1_bytes, W1_scale, g, 
             nc.sync.dma_start(out=b_wide[c][:], in_=b[c * SPAN : (c + 1) * SPAN].partition_broadcast(P))
 
         def widen(on, u, j):
-            scale = s1[:, u % 4, j : j + 1] if u < 8 else s2[:, u % 2, j : j + 1]
+            scale = (s0[:, 0] if u == 0 else s1[:, u - 1] if u < 4 else s2[:, u % 2])[:, j : j + 1]
             if u not in wide:
-                if u < 8:
-                    wide[u] = ring("wide1_", u, 3, [P, PACK, SPAN], BF16)
-                else:
-                    wide[u] = ring("wide2_", u - 8, 3, [P, PACK, 2 * SPAN], BF16)
+                wide[u] = ring("wide", u, 4, [P, PACK, 2 * SPAN], BF16)
             src = raw[u][:, j, :].bitcast(FP8)
             if on == "S":
                 nc.scalar.activation(out=wide[u][:, j, :], in_=src, func=ACT.Copy, scale=scale)
@@ -142,15 +111,18 @@ def tile_pointwise_bottleneck_hardswish_d5_kernel(tc, x, W1_bytes, W1_scale, g, 
                 )
 
         def weave(on, u):
-            woven[u] = ring("woven", u, 3, [P, SPAN * PACK], BF16)
-            if u < 8:
+            which, k, c = pieces[u]
+            src = wide[load_of(u)][:, :, c % 2 * SPAN : (c % 2 + 1) * SPAN]
+            if which == 1:
+                woven[u] = ring("woven", len(woven), 3, [P, SPAN * PACK], BF16)
                 nc.vector.tensor_copy(
                     out=woven[u][:].rearrange("p (t a m j) -> p a t m j", t=PACK, m=2, j=PACK),
-                    in_=wide[u][:].rearrange("p j (a m t) -> p a t m j", m=2, t=PACK),
+                    in_=src.rearrange("p j (a m t) -> p a t m j", m=2, t=PACK),
                 )
             else:
-                side = pieces[u][2] % 2
-                interleave(on, woven[u][:], wide[load_of(u)][:, :, side * SPAN : (side + 1) * SPAN])
+                if u - k not in woven:
+                    woven[u - k] = ring("xwoven", c, 2, [P, 2, SPAN * PACK], BF16) if c < 2 else ring("hwoven", 0, 1, [P, 2, SPAN * PACK], BF16)
+                interleave(on, woven[u - k][:, k, :], src)
 
         def quantize(name, src, words):
             codes = keep.tile([P, words], U32, name=name + "_codes", align_bytes=64)
@@ -159,7 +131,14 @@ def tile_pointwise_bottleneck_hardswish_d5_kernel(tc, x, W1_bytes, W1_scale, g, 
             return codes, scales
 
         def quant_piece(on, u):
-            w_codes[pieces[u]], w_scales[pieces[u]] = quantize("w%d" % u, woven[u][:], SPAN)
+            which, k, c = pieces[u]
+            if which == 1:
+                codes, scales = quantize("w%d" % u, woven[u][:], SPAN)
+                w_codes[1, k, c], w_scales[1, k, c] = codes[:], scales[:]
+            else:
+                codes, scales = quantize("w%d" % u, woven[u][:].rearrange("p k n -> p (k n)"), 2 * SPAN)
+                for k in range(2):
+                    w_codes[2, k, c], w_scales[2, k, c] = codes[:, k * SPAN : (k + 1) * SPAN], scales[:, k * SPAN : (k + 1) * SPAN]
 
         def x_turn(on, i, pair):
             words = x_sb[i][:].bitcast(F32)
@@ -181,8 +160,10 @@ def tile_pointwise_bottleneck_hardswish_d5_kernel(tc, x, W1_bytes, W1_scale, g, 
             else:
                 nc.vector.tensor_copy(out=words, in_=src)
 
-        def x_quant(on, hf, k):
-            x_codes[hf, k], x_scales[hf, k] = quantize("x%d%d" % (hf, k), x_woven[hf, k // 2][:, k % 2, :], SPAN)
+        def x_quant(on, hf, pair):
+            codes, scales = quantize("x%d%d" % (hf, pair), x_woven[hf, pair][:].rearrange("p k n -> p (k n)"), 2 * SPAN)
+            for k in range(2):
+                x_codes[hf, 2 * pair + k], x_scales[hf, 2 * pair + k] = codes[:, k * SPAN : (k + 1) * SPAN], scales[:, k * SPAN : (k + 1) * SPAN]
 
         def mx(dst, lhs_c, lhs_s, rhs_c, rhs_s, start, stop):
             nc.tensor.matmul_mx(out=dst, lhsT=lhs_c.bitcast(FP8X4), lhsT_scale=lhs_s, rhs=rhs_c.bitcast(FP8X4), rhs_scale=rhs_s, start=start, stop=stop)
@@ -203,11 +184,14 @@ def tile_pointwise_bottleneck_hardswish_d5_kernel(tc, x, W1_bytes, W1_scale, g, 
                 nc.vector.tensor_scalar(out=h_rows[hf, c][:, t, :], in0=y_bank[hf, c, t][:], scalar1=g_col[:, c, t : t + 1], scalar2=None, op0=ALU.mult)
 
         def h_weave(on, hf, c):
-            h_woven[hf, c] = ring("hwoven", c, 2, [P, SPAN * PACK], BF16)
-            interleave(on, h_woven[hf, c][:], h_rows[hf, c][:])
+            if hf not in h_woven:
+                h_woven[hf] = ring("hwoven", 0, 1, [P, 2, SPAN * PACK], BF16)
+            interleave(on, h_woven[hf][:, c, :], h_rows[hf, c][:])
 
-        def h_quant(on, hf, c):
-            h_codes[hf, c], h_scales[hf, c] = quantize("h%d%d" % (hf, c), h_woven[hf, c][:], SPAN)
+        def h_quant(on, hf):
+            codes, scales = quantize("h%d" % hf, h_woven[hf][:].rearrange("p k n -> p (k n)"), 2 * SPAN)
+            for k in range(2):
+                h_codes[hf, k], h_scales[hf, k] = codes[:, k * SPAN : (k + 1) * SPAN], scales[:, k * SPAN : (k + 1) * SPAN]
 
         def g_copy(on):
             nc.vector.tensor_copy(out=g_col[:], in_=g_sb[:])
@@ -274,7 +258,9 @@ def tile_pointwise_bottleneck_hardswish_d5_kernel(tc, x, W1_bytes, W1_scale, g, 
         h_rows = {}
         b_bank = {}
 
-        nc.scalar.dma_start(out=s1[:], in_=W1_scale.rearrange("(k p j) o -> p k (j o)", p=P, j=PACK))
+        by_row = W1_scale.rearrange("(k p j) o -> p k (j o)", p=P, j=PACK)
+        nc.sync.dma_start(out=s0[:], in_=by_row[:, :1])
+        nc.scalar.dma_start(out=s1[:], in_=by_row[:, 1:])
         load_piece(0)
         load_piece(1)
         load_x(0)
@@ -284,13 +270,11 @@ def tile_pointwise_bottleneck_hardswish_d5_kernel(tc, x, W1_bytes, W1_scale, g, 
         load_x(2)
         load_x(3)
         nc.sync.dma_start(out=g_sb[:], in_=g.rearrange("(k p j) -> p k j", p=P, j=PACK))
-        for u in range(4, 8):
-            load_piece(u)
         nc.sync.dma_start(out=s2[:], in_=W2_scale.rearrange("(k p j) o -> p k (j o)", p=P, j=PACK))
         nc.sync.dma_start(out=b_rows[:], in_=b.rearrange("(q n) -> q n", n=P))
         for i in range(4, 8):
             load_x(i)
-        for u in range(8, 12):
+        for u in range(4, 8):
             load_piece(u)
         for c in sorted(set(outs[e][0] for e in DIRECT)):
             load_b_wide(c)
@@ -310,11 +294,113 @@ def tile_pointwise_bottleneck_hardswish_d5_kernel(tc, x, W1_bytes, W1_scale, g, 
         def b_columns(on):
             nc.scalar.copy(out=b_col[:], in_=b_bank[0][:, : COUT // P])
 
-        steps = {
-            "widen": widen, "weave": weave, "wq": quant_piece, "xturn": x_turn, "xcopy": x_copy, "xq": x_quant,
-            "mm1": mm1, "hs": h_scale, "hw": h_weave, "hq": h_quant, "gcopy": g_copy, "mm2": mm2, "bias": add_bias, "turn": turn_back, "gate": gate,
-            "fin": finish, "store": store, "bcopy": b_copy, "bturn": b_turn, "bcol": b_columns,
-        }
-        for entry in ORDER.split():
-            parts = entry.split(".")
-            steps[parts[0]](parts[1], *[int(a) for a in parts[2:]])
+        def rows(on, l):
+            for j in range(PACK):
+                if (j >= PACK - V_ROWS[l]) == (on == "V"):
+                    widen(on, l, j)
+
+        def both(fn, on, i):
+            fn(on, i, 0)
+            fn(on, i, 1)
+
+        for l in range(4):
+            rows("S", l)
+        rows("V", 0)
+        rows("V", 1)
+        for pair in range(2):
+            for i in range(4):
+                x_turn("P", i, pair)
+        weave("V", 0)
+        weave("V", 1)
+        rows("V", 2)
+        quant_piece("V", 0)
+        weave("V", 4)
+        quant_piece("V", 1)
+        rows("V", 3)
+        weave("V", 2)
+        quant_piece("V", 4)
+        weave("V", 5)
+        quant_piece("V", 2)
+        g_copy("V")
+        b_copy("V")
+        weave("V", 3)
+        for pair in range(2):
+            for i in range(4):
+                x_copy("S", i, pair)
+        for pair in range(2):
+            for i in range(4, 8):
+                x_turn("P", i, pair)
+        x_quant("V", 0, 0)
+        quant_piece("V", 3)
+        x_quant("V", 0, 1)
+        quant_piece("V", 5)
+        weave("V", 6)
+        weave("V", 7)
+        widen("S", 4, 0)
+        for i in range(4, 8):
+            x_copy("S", i, 0)
+        for t in range(4):
+            mm1("P", 0, 0, t)
+        widen("S", 4, 1)
+        for i in range(4, 8):
+            x_copy("S", i, 1)
+        widen("S", 4, 2)
+        quant_piece("V", 6)
+        quant_piece("V", 7)
+        rows("V", 4)
+        rows("V", 5)
+        for t in range(4):
+            h_scale("S", 0, 0, t)
+            mm1("P", 0, 1, t)
+        rows("S", 5)
+        x_quant("V", 1, 0)
+        x_quant("V", 1, 1)
+        h_weave("V", 0, 0)
+        weave("V", 8)
+        for t in range(4):
+            mm1("P", 1, 0, t)
+            h_scale("S", 0, 1, t)
+        b_turn("P")
+        weave("V", 9)
+        h_weave("V", 0, 1)
+        quant_piece("V", 8)
+        h_quant("V", 0)
+        weave("V", 10)
+        weave("V", 11)
+        rows("S", 6)
+        for t in range(4):
+            h_scale("S", 1, 0, t)
+            mm1("P", 1, 1, t)
+        rows("V", 6)
+        quant_piece("V", 10)
+        b_columns("S")
+        rows("S", 7)
+        for t in range(4):
+            mm2("P", 0, t)
+            h_scale("S", 1, 1, t)
+        h_weave("V", 1, 0)
+        for q in range(4):
+            add_bias("S", 0, q)
+            mm2("P", 1, q)
+        h_weave("V", 1, 1)
+        rows("V", 7)
+        h_quant("V", 1)
+        for e in range(8):
+            nxt = e + 1
+            for r in range(4):
+                turn_back("P", e, r)
+            if e in (0, 2):
+                weave("G", 12 + e)
+                weave("G", 13 + e)
+            for q in range(4):
+                if nxt < 8:
+                    add_bias("V" if q >= 4 - V_BIAS[nxt] else "S", nxt, q)
+            if e + 2 < 8:
+                for q in range(4):
+                    mm2("P", e + 2, q)
+            for r in range(4):
+                gate("S", e, r)
+                finish("V", e, r)
+                store("D", e, r)
+                if r == QAT[min(e // 2, 1)] and e in (1, 3):
+                    quant_piece("V", 11 + e)

@@ -23,9 +23,10 @@ BANKS = 8
 DIRECT = ()
 WIDEU = ()
 OUTS = ((0, 0), (1, 0), (0, 1), (1, 1), (2, 0), (2, 1), (3, 0), (3, 1))
-V_ROWS = [2,2,1,1,1,2,2,2]
+V_ROWS = [0, 0, 0, 0, 0, 0, 1, 3]
 V_BIAS = [0, 2, 2, 1, 2, 2, 2, 2]
 QAT = [3, 3]
+W_ON = [1, 1, 0, 0]
 FAST = True
 
 
@@ -76,7 +77,7 @@ def tile_pointwise_bottleneck_hardswish_d5_kernel(tc, x, W1_bytes, W1_scale, g, 
             src = src.rearrange("(p j) n -> p j n", j=PACK)
             raw[l] = keep.tile([P, PACK, 2 * SPAN], U8, name="raw%d" % l, align_bytes=64)
             if l == 0:
-                for j in range(PACK):
+                for j in (3, 0, 2, 1):
                     nc.sync.dma_start(out=raw[l][:, j, :], in_=src[:, j, :])
             else:
                 nc.sync.dma_start(out=raw[l][:], in_=src)
@@ -89,15 +90,32 @@ def tile_pointwise_bottleneck_hardswish_d5_kernel(tc, x, W1_bytes, W1_scale, g, 
             b_wide[c] = keep.tile([P, SPAN], BF16, name="b_wide%d" % c, align_bytes=64)
             nc.sync.dma_start(out=b_wide[c][:], in_=b[c * SPAN : (c + 1) * SPAN].partition_broadcast(P))
 
-        def widen(on, u, j):
+        def paired(l, c):
+            return (l < 4 and c == 1) or l in (4, 5)
+
+        def wide_view(l, c):
+            if l not in wide:
+                wide[l] = ring("wide", l, 4, [P, 2 * PACK * SPAN], BF16)
+            flat = wide[l][:, c * PACK * SPAN : (c + 1) * PACK * SPAN] if l < 4 else wide[l][:]
+            if paired(l, c):
+                return flat.rearrange("p (u n e) -> p u n e", u=2, e=2)
+            return flat.rearrange("p (j n) -> p j n", j=PACK)
+
+        def widen(on, u, j, c=0):
             scale = (s0[:, 0] if u == 0 else s1[:, u - 1] if u < 4 else s2[:, u % 2])[:, j : j + 1]
-            if u not in wide:
-                wide[u] = ring("wide", u, 4, [P, PACK, 2 * SPAN], BF16)
-            src = raw[u][:, j, :].bitcast(FP8)
+            src = (raw[u][:, j, c * SPAN : (c + 1) * SPAN] if u < 4 else raw[u][:, j, :]).bitcast(FP8)
+            view = wide_view(u, c)
+            dst = view[:, j // 2, :, j % 2] if paired(u, c) else view[:, j, :]
             if on == "S":
-                nc.scalar.activation(out=wide[u][:, j, :], in_=src, func=ACT.Copy, scale=scale)
+                nc.scalar.activation(out=dst, in_=src, func=ACT.Copy, scale=scale)
             else:
-                nc.vector.tensor_scalar(out=wide[u][:, j, :], in0=src, scalar1=scale, scalar2=None, op0=ALU.mult)
+                nc.vector.tensor_scalar(out=dst, in0=src, scalar1=scale, scalar2=None, op0=ALU.mult)
+
+        def move(on, dst, src):
+            if on == "S":
+                nc.scalar.copy(out=dst, in_=src)
+            else:
+                nc.vector.tensor_copy(out=dst, in_=src)
 
         def interleave(on, dst, src):
             if on == "V" and FAST:
@@ -112,17 +130,27 @@ def tile_pointwise_bottleneck_hardswish_d5_kernel(tc, x, W1_bytes, W1_scale, g, 
 
         def weave(on, u):
             which, k, c = pieces[u]
-            src = wide[load_of(u)][:, :, c % 2 * SPAN : (c % 2 + 1) * SPAN]
+            l = load_of(u)
+            view = wide_view(l, c if which == 1 else 0)
             if which == 1:
-                woven[u] = ring("woven", len(woven), 3, [P, SPAN * PACK], BF16)
-                nc.vector.tensor_copy(
-                    out=woven[u][:].rearrange("p (t a m j) -> p a t m j", t=PACK, m=2, j=PACK),
-                    in_=src.rearrange("p j (a m t) -> p a t m j", m=2, t=PACK),
-                )
+                woven[u] = ring("woven", len(woven), 4, [P, SPAN * PACK], BF16)
+                if c == 0:
+                    nc.vector.tensor_copy(
+                        out=woven[u][:].rearrange("p (t a m j) -> p a t m j", t=PACK, m=2, j=PACK),
+                        in_=view.rearrange("p j (a m t) -> p a t m j", m=2, t=PACK),
+                    )
+                else:
+                    words = view.rearrange("p u n e -> p u (n e)").bitcast(F32)
+                    move(on, woven[u][:].bitcast(F32).rearrange("p (t a m u) -> p a t m u", t=PACK, m=2, u=2), words.rearrange("p u (a m t) -> p a t m u", m=2, t=PACK))
+                return
+            if u - k not in woven:
+                woven[u - k] = ring("xwoven", c, 2, [P, 2, SPAN * PACK], BF16) if c < 2 else ring("hwoven", 0, 1, [P, 2, SPAN * PACK], BF16)
+            cols = slice(c % 2 * SPAN, (c % 2 + 1) * SPAN)
+            if c < 2:
+                words = view.rearrange("p u n e -> p u (n e)").bitcast(F32)[:, :, cols]
+                move(on, woven[u - k][:, k, :].bitcast(F32).rearrange("p (n u) -> p n u", u=2), words.rearrange("p u n -> p n u"))
             else:
-                if u - k not in woven:
-                    woven[u - k] = ring("xwoven", c, 2, [P, 2, SPAN * PACK], BF16) if c < 2 else ring("hwoven", 0, 1, [P, 2, SPAN * PACK], BF16)
-                interleave(on, woven[u - k][:, k, :], src)
+                interleave(on, woven[u - k][:, k, :], view[:, :, cols])
 
         def quantize(name, src, words):
             codes = keep.tile([P, words], U32, name=name + "_codes", align_bytes=64)
@@ -239,42 +267,37 @@ def tile_pointwise_bottleneck_hardswish_d5_kernel(tc, x, W1_bytes, W1_scale, g, 
         def z_of(e, r):
             return part("zt", 0, 4, e, r) if e in DIRECT else z_src[e, r]
 
-        def gate(on, e, r):
-            nc.scalar.activation(out=part("gate", 4, 2, e, r), in_=z_of(e, r), func=ACT.Relu, bias=half[:], scale=1.0 / 6.0)
+        def gate(on, e, r, cols=slice(0, SPAN)):
+            nc.scalar.activation(out=part("gate", 4, 2, e, r)[:, cols], in_=z_of(e, r)[:, cols], func=ACT.Relu, bias=half[:], scale=1.0 / 6.0)
 
-        def finish(on, e, r):
-            nc.vector.scalar_tensor_tensor(out=part("res", 6, 3, e, r), in0=part("gate", 4, 2, e, r), scalar=1.0, in1=z_of(e, r), op0=ALU.min, op1=ALU.mult)
+        def finish(on, e, r, cols=slice(0, SPAN)):
+            nc.vector.scalar_tensor_tensor(out=part("res", 6, 3, e, r)[:, cols], in0=part("gate", 4, 2, e, r)[:, cols], scalar=1.0, in1=z_of(e, r)[:, cols], op0=ALU.min, op1=ALU.mult)
 
-        def store(on, e, r):
+        def store(on, e, r, cols=slice(0, SPAN)):
             c, hf = outs[e]
             i = 4 * hf + r
-            cols = slice(c * SPAN, (c + 1) * SPAN)
-            if e in WIDEU:
-                nc.sync.dma_start(out=out[i * P : (i + 2) * P, cols].rearrange("(a p) n -> p a n", p=P), in_=pair_tile("res", 6, 3, e, r)[:])
-            else:
-                nc.sync.dma_start(out=out[i * P : (i + 1) * P, cols], in_=part("res", 6, 3, e, r))
+            nc.sync.dma_start(out=out[i * P : (i + 1) * P, c * SPAN + cols.start : c * SPAN + cols.stop], in_=part("res", 6, 3, e, r)[:, cols])
 
         outs = OUTS
         h_rows = {}
         b_bank = {}
 
         by_row = W1_scale.rearrange("(k p j) o -> p k (j o)", p=P, j=PACK)
-        nc.sync.dma_start(out=s0[:], in_=by_row[:, :1])
-        nc.scalar.dma_start(out=s1[:], in_=by_row[:, 1:])
+        nc.scalar.dma_start(out=s0[:], in_=by_row[:, :1])
         load_piece(0)
+        nc.sync.dma_start(out=s1[:], in_=by_row[:, 1:])
         load_piece(1)
         load_x(0)
         load_piece(2)
         load_x(1)
         load_piece(3)
-        load_x(2)
-        load_x(3)
+        for i in range(2, 8):
+            load_x(i)
         nc.sync.dma_start(out=g_sb[:], in_=g.rearrange("(k p j) -> p k j", p=P, j=PACK))
         nc.sync.dma_start(out=s2[:], in_=W2_scale.rearrange("(k p j) o -> p k (j o)", p=P, j=PACK))
+        load_piece(4)
         nc.sync.dma_start(out=b_rows[:], in_=b.rearrange("(q n) -> q n", n=P))
-        for i in range(4, 8):
-            load_x(i)
-        for u in range(4, 8):
+        for u in range(5, 8):
             load_piece(u)
         for c in sorted(set(outs[e][0] for e in DIRECT)):
             load_b_wide(c)
@@ -294,101 +317,95 @@ def tile_pointwise_bottleneck_hardswish_d5_kernel(tc, x, W1_bytes, W1_scale, g, 
         def b_columns(on):
             nc.scalar.copy(out=b_col[:], in_=b_bank[0][:, : COUT // P])
 
-        def rows(on, l):
-            for j in range(PACK):
-                if (j >= PACK - V_ROWS[l]) == (on == "V"):
-                    widen(on, l, j)
-
-        def both(fn, on, i):
-            fn(on, i, 0)
-            fn(on, i, 1)
+        def rows(on, l, c=0, js=range(PACK)):
+            for j in js:
+                widen(on, l, j, c)
 
         for l in range(4):
-            rows("S", l)
-        rows("V", 0)
-        rows("V", 1)
+            rows("S", l, 0)
+        rows("V", 0, 1)
+        rows("V", 1, 1)
         for pair in range(2):
             for i in range(4):
                 x_turn("P", i, pair)
         weave("V", 0)
         weave("V", 1)
-        rows("V", 2)
+        rows("V", 2, 1, (0, 1))
         quant_piece("V", 0)
-        weave("V", 4)
         quant_piece("V", 1)
-        rows("V", 3)
         weave("V", 2)
-        quant_piece("V", 4)
-        weave("V", 5)
-        quant_piece("V", 2)
-        g_copy("V")
-        b_copy("V")
+        rows("V", 2, 1, (2, 3))
+        for i in range(4):
+            x_copy("S", i, 0)
         weave("V", 3)
-        for pair in range(2):
-            for i in range(4):
-                x_copy("S", i, pair)
-        for pair in range(2):
-            for i in range(4, 8):
-                x_turn("P", i, pair)
+        quant_piece("V", 2)
+        for i in range(4):
+            x_copy("S", i, 1)
+        for i in range(4, 8):
+            x_turn("P", i, 0)
         x_quant("V", 0, 0)
         quant_piece("V", 3)
         x_quant("V", 0, 1)
-        quant_piece("V", 5)
-        weave("V", 6)
-        weave("V", 7)
-        widen("S", 4, 0)
-        for i in range(4, 8):
-            x_copy("S", i, 0)
         for t in range(4):
             mm1("P", 0, 0, t)
-        widen("S", 4, 1)
+        weave("S", 4)
+        rows("V", 3, 1)
         for i in range(4, 8):
-            x_copy("S", i, 1)
-        widen("S", 4, 2)
-        quant_piece("V", 6)
+            x_copy("S", i, 0)
+            x_turn("P", i, 1)
+        weave("SV"[W_ON[3]], 5)
+        weave("S", 6)
+        weave("SV"[W_ON[0]], 7)
+        quant_piece("V", 4)
+        g_copy("V")
         quant_piece("V", 7)
+        quant_piece("V", 5)
+        quant_piece("V", 6)
+        b_copy("V")
         rows("V", 4)
-        rows("V", 5)
         for t in range(4):
             h_scale("S", 0, 0, t)
             mm1("P", 0, 1, t)
-        rows("S", 5)
+        for i in range(4, 8):
+            x_copy("S", i, 1)
         x_quant("V", 1, 0)
         x_quant("V", 1, 1)
-        h_weave("V", 0, 0)
-        weave("V", 8)
+        rows("V", 5)
+        rows("S", 6, 0, range(PACK - V_ROWS[6]))
         for t in range(4):
             mm1("P", 1, 0, t)
             h_scale("S", 0, 1, t)
         b_turn("P")
-        weave("V", 9)
+        h_weave("V", 0, 0)
+        weave("SV"[W_ON[2]], 8)
+        weave("S", 9)
         h_weave("V", 0, 1)
-        quant_piece("V", 8)
+        weave("SV"[W_ON[1]], 10)
+        rows("V", 6, 0, range(PACK - V_ROWS[6], PACK))
         h_quant("V", 0)
-        weave("V", 10)
-        weave("V", 11)
-        rows("S", 6)
+        quant_piece("V", 8)
         for t in range(4):
             h_scale("S", 1, 0, t)
             mm1("P", 1, 1, t)
-        rows("V", 6)
-        quant_piece("V", 10)
+        weave("S", 11)
         b_columns("S")
-        rows("S", 7)
         for t in range(4):
             mm2("P", 0, t)
             h_scale("S", 1, 1, t)
         h_weave("V", 1, 0)
+        quant_piece("V", 10)
+        rows("S", 7, 0, range(PACK - V_ROWS[7]))
         for q in range(4):
             add_bias("S", 0, q)
             mm2("P", 1, q)
         h_weave("V", 1, 1)
-        rows("V", 7)
+        rows("V", 7, 0, range(PACK - V_ROWS[7], PACK))
         h_quant("V", 1)
         for e in range(8):
             nxt = e + 1
             for r in range(4):
-                turn_back("P", e, r)
+                if e not in DIRECT:
+                    turn_back("P", e, r)
             if e in (0, 2):
                 weave("G", 12 + e)
                 weave("G", 13 + e)
@@ -400,7 +417,12 @@ def tile_pointwise_bottleneck_hardswish_d5_kernel(tc, x, W1_bytes, W1_scale, g, 
                     mm2("P", e + 2, q)
             for r in range(4):
                 gate("S", e, r)
-                finish("V", e, r)
-                store("D", e, r)
+                if (e, r) == (7, 3):
+                    for cols in (slice(0, SPAN // 2), slice(SPAN // 2, SPAN)):
+                        finish("V", e, r, cols)
+                        store("D", e, r, cols)
+                else:
+                    finish("V", e, r)
+                    store("D", e, r)
                 if r == QAT[min(e // 2, 1)] and e in (1, 3):
                     quant_piece("V", 11 + e)

from contextlib import ExitStack

import concourse.mybir as mybir
from concourse.masks import make_identity

PIX, CIN, MID, COUT = 1024, 2048, 1024, 2048
FLOPS = 2 * PIX * CIN * MID + 2 * PIX * MID * COUT

F32 = mybir.dt.float32
BF16 = mybir.dt.bfloat16
U32 = mybir.dt.uint32
U8 = mybir.dt.uint8
FP8 = mybir.dt.float8_e4m3fn
FP8X4 = mybir.dt.float8_e4m3fn_x4
ALU = mybir.AluOpType
ACT = mybir.ActivationFunctionType

P = 128
PACK = 4
SPAN = P * PACK
BANKS = 8

DIRECT = ()
WIDEU = ()
OUTS = ((0, 0), (1, 0), (0, 1), (1, 1), (2, 0), (2, 1), (3, 0), (3, 1))
V_ROWS = [0, 0, 0, 0, 0, 0, 1, 3]
V_BIAS = [0, 2, 2, 1, 2, 2, 2, 2]
QAT = [3, 3]
W_ON = [1, 1, 0, 0]
FAST = True


def tile_pointwise_bottleneck_hardswish_d5_kernel(tc, x, W1_bytes, W1_scale, g, W2_bytes, W2_scale, b, out):
    nc = tc.nc
    with ExitStack() as ctx:
        keep = ctx.enter_context(tc.tile_pool(name="keep", bufs=1))
        psum = ctx.enter_context(tc.psum_pool(name="psum", bufs=1))
        ctx.enter_context(tc.manual_schedule())

        filled = []

        def next_bank(shape):
            bank = psum.tile(shape, F32, name="bank%d" % (len(filled) % BANKS))
            filled.append(bank)
            return bank

        def ring(kind, n, depth, shape, dtype):
            return keep.tile(shape, dtype, name="%s%d" % (kind, n % depth), align_bytes=64)

        ident = keep.tile([P, P], F32, name="ident")
        s0 = keep.tile([P, 1, PACK], F32, name="s0")
        s1 = keep.tile([P, CIN // SPAN - 1, PACK], F32, name="s1")
        s2 = keep.tile([P, MID // SPAN, PACK], F32, name="s2")
        g_sb = keep.tile([P, MID // SPAN, PACK], BF16, name="g_sb")
        g_col = keep.tile([P, MID // SPAN, PACK], F32, name="g_col")
        b_rows = keep.tile([COUT // P, P], BF16, name="b_rows")
        b_sq = keep.tile([P, P], F32, name="b_sq")
        b_col = keep.tile([P, COUT // P], F32, name="b_col")
        half = keep.tile([P, 1], F32, name="half")
        warm = keep.tile([P, 1], F32, name="warm")

        pieces = [(1, k, c) for c in range(2) for k in range(4)] + [(2, k, c) for c in range(4) for k in range(2)]
        raw, wide, woven, w_codes, w_scales = {}, {}, {}, {}, {}
        x_sb, x_banks, x_woven, x_codes, x_scales = {}, {}, {}, {}, {}
        y_bank, h_woven, h_codes, h_scales = {}, {}, {}, {}
        zt_bank, zt_sb, z_src, gate_sb, b_wide = {}, {}, {}, {}, {}

        def load_of(u):
            return u % 4 if u < 8 else 4 + 2 * ((u - 8) // 4) + u % 2

        def load_piece(l):
            if l < 4:
                src = W1_bytes[l * SPAN : (l + 1) * SPAN, :]
            else:
                k, pair = l % 2, (l - 4) // 2
                src = W2_bytes[k * SPAN : (k + 1) * SPAN, pair * 2 * SPAN : (pair + 1) * 2 * SPAN]
            src = src.rearrange("(p j) n -> p j n", j=PACK)
            raw[l] = keep.tile([P, PACK, 2 * SPAN], U8, name="raw%d" % l, align_bytes=64)
            if l == 0:
                for j in (3, 0, 2, 1):
                    nc.sync.dma_start(out=raw[l][:, j, :], in_=src[:, j, :])
            else:
                nc.sync.dma_start(out=raw[l][:], in_=src)

        def load_x(i):
            x_sb[i] = keep.tile([P, CIN], BF16, name="slot%d" % i, align_bytes=64)
            nc.sync.dma_start(out=x_sb[i][:], in_=x[i * P : (i + 1) * P, :])

        def load_b_wide(c):
            b_wide[c] = keep.tile([P, SPAN], BF16, name="b_wide%d" % c, align_bytes=64)
            nc.sync.dma_start(out=b_wide[c][:], in_=b[c * SPAN : (c + 1) * SPAN].partition_broadcast(P))

        def paired(l, c):
            return (l < 4 and c == 1) or l in (4, 5)

        def wide_view(l, c):
            if l not in wide:
                wide[l] = ring("wide", l, 4, [P, 2 * PACK * SPAN], BF16)
            flat = wide[l][:, c * PACK * SPAN : (c + 1) * PACK * SPAN] if l < 4 else wide[l][:]
            if paired(l, c):
                return flat.rearrange("p (u n e) -> p u n e", u=2, e=2)
            return flat.rearrange("p (j n) -> p j n", j=PACK)

        def widen(on, u, j, c=0):
            scale = (s0[:, 0] if u == 0 else s1[:, u - 1] if u < 4 else s2[:, u % 2])[:, j : j + 1]
            src = (raw[u][:, j, c * SPAN : (c + 1) * SPAN] if u < 4 else raw[u][:, j, :]).bitcast(FP8)
            view = wide_view(u, c)
            dst = view[:, j // 2, :, j % 2] if paired(u, c) else view[:, j, :]
            if on == "S":
                nc.scalar.activation(out=dst, in_=src, func=ACT.Copy, scale=scale)
            else:
                nc.vector.tensor_scalar(out=dst, in0=src, scalar1=scale, scalar2=None, op0=ALU.mult)

        def move(on, dst, src):
            if on == "S":
                nc.scalar.copy(out=dst, in_=src)
            else:
                nc.vector.tensor_copy(out=dst, in_=src)

        def interleave(on, dst, src):
            if on == "V" and FAST:
                nc.vector.tensor_copy(out=dst.rearrange("p (c i j) -> p c j i", i=4, j=PACK), in_=src.rearrange("p j (c i) -> p c j i", i=4))
            elif on == "V":
                nc.vector.tensor_copy(out=dst.rearrange("p (n j) -> p n j", j=PACK), in_=src.rearrange("p j n -> p n j"))
            else:
                nc.gpsimd.tensor_scalar(
                    out=dst.rearrange("p (n j) -> p n j", j=PACK), in0=src.rearrange("p j n -> p n j"),
                    scalar1=1.0, scalar2=0.0, op0=ALU.mult, op1=ALU.add,
                )

        def weave(on, u):
            which, k, c = pieces[u]
            l = load_of(u)
            view = wide_view(l, c if which == 1 else 0)
            if which == 1:
                woven[u] = ring("woven", len(woven), 4, [P, SPAN * PACK], BF16)
                if c == 0:
                    nc.vector.tensor_copy(
                        out=woven[u][:].rearrange("p (t a m j) -> p a t m j", t=PACK, m=2, j=PACK),
                        in_=view.rearrange("p j (a m t) -> p a t m j", m=2, t=PACK),
                    )
                else:
                    words = view.rearrange("p u n e -> p u (n e)").bitcast(F32)
                    move(on, woven[u][:].bitcast(F32).rearrange("p (t a m u) -> p a t m u", t=PACK, m=2, u=2), words.rearrange("p u (a m t) -> p a t m u", m=2, t=PACK))
                return
            if u - k not in woven:
                woven[u - k] = ring("xwoven", c, 2, [P, 2, SPAN * PACK], BF16) if c < 2 else ring("hwoven", 0, 1, [P, 2, SPAN * PACK], BF16)
            cols = slice(c % 2 * SPAN, (c % 2 + 1) * SPAN)
            if c < 2:
                words = view.rearrange("p u n e -> p u (n e)").bitcast(F32)[:, :, cols]
                move(on, woven[u - k][:, k, :].bitcast(F32).rearrange("p (n u) -> p n u", u=2), words.rearrange("p u n -> p n u"))
            else:
                interleave(on, woven[u - k][:, k, :], view[:, :, cols])

        def quantize(name, src, words):
            codes = keep.tile([P, words], U32, name=name + "_codes", align_bytes=64)
            scales = keep.tile([P, words], U8, name=name + "_scales", align_bytes=64)
            nc.vector.quantize_mx(out=codes[:].bitcast(FP8X4), scales=scales[:], in_=src)
            return codes, scales

        def quant_piece(on, u):
            which, k, c = pieces[u]
            if which == 1:
                codes, scales = quantize("w%d" % u, woven[u][:], SPAN)
                w_codes[1, k, c], w_scales[1, k, c] = codes[:], scales[:]
            else:
                codes, scales = quantize("w%d" % u, woven[u][:].rearrange("p k n -> p (k n)"), 2 * SPAN)
                for k in range(2):
                    w_codes[2, k, c], w_scales[2, k, c] = codes[:, k * SPAN : (k + 1) * SPAN], scales[:, k * SPAN : (k + 1) * SPAN]

        def x_turn(on, i, pair):
            words = x_sb[i][:].bitcast(F32)
            bank = next_bank([P, 2, 2, P])
            x_banks[i, pair] = bank
            for k2 in range(2):
                k = 2 * pair + k2
                for u in range(2):
                    nc.tensor.transpose(bank[:, k2, u, :], words[:, 256 * k + u : 256 * (k + 1) : 2], ident[:])

        def x_copy(on, i, pair):
            key = (i // 4, pair)
            if key not in x_woven:
                x_woven[key] = ring("xwoven", pair, 2, [P, 2, SPAN * PACK], BF16)
            words = x_woven[key][:].bitcast(F32).rearrange("p k (i r u) -> p k i r u", i=4, u=2)[:, :, i % 4]
            src = x_banks[i, pair][:].rearrange("p k u r -> p k r u")
            if on == "S":
                nc.scalar.copy(out=words, in_=src)
            else:
                nc.vector.tensor_copy(out=words, in_=src)

        def x_quant(on, hf, pair):
            codes, scales = quantize("x%d%d" % (hf, pair), x_woven[hf, pair][:].rearrange("p k n -> p (k n)"), 2 * SPAN)
            for k in range(2):
                x_codes[hf, 2 * pair + k], x_scales[hf, 2 * pair + k] = codes[:, k * SPAN : (k + 1) * SPAN], scales[:, k * SPAN : (k + 1) * SPAN]

        def mx(dst, lhs_c, lhs_s, rhs_c, rhs_s, start, stop):
            nc.tensor.matmul_mx(out=dst, lhsT=lhs_c.bitcast(FP8X4), lhsT_scale=lhs_s, rhs=rhs_c.bitcast(FP8X4), rhs_scale=rhs_s, start=start, stop=stop)

        def mm1(on, hf, c, t):
            bank = next_bank([P, SPAN])
            y_bank[hf, c, t] = bank
            ch = slice(t * P, (t + 1) * P)
            for k in range(4):
                mx(bank[:], w_codes[1, k, c][:, ch], w_scales[1, k, c][:, ch], x_codes[hf, k][:], x_scales[hf, k][:], k == 0, k == 3)

        def h_scale(on, hf, c, t):
            if (hf, c) not in h_rows:
                h_rows[hf, c] = ring("hrows", c, 2, [P, PACK, SPAN], BF16)
            if on == "S":
                nc.scalar.activation(out=h_rows[hf, c][:, t, :], in_=y_bank[hf, c, t][:], func=ACT.Copy, scale=g_col[:, c, t : t + 1])
            else:
                nc.vector.tensor_scalar(out=h_rows[hf, c][:, t, :], in0=y_bank[hf, c, t][:], scalar1=g_col[:, c, t : t + 1], scalar2=None, op0=ALU.mult)

        def h_weave(on, hf, c):
            if hf not in h_woven:
                h_woven[hf] = ring("hwoven", 0, 1, [P, 2, SPAN * PACK], BF16)
            interleave(on, h_woven[hf][:, c, :], h_rows[hf, c][:])

        def h_quant(on, hf):
            codes, scales = quantize("h%d" % hf, h_woven[hf][:].rearrange("p k n -> p (k n)"), 2 * SPAN)
            for k in range(2):
                h_codes[hf, k], h_scales[hf, k] = codes[:, k * SPAN : (k + 1) * SPAN], scales[:, k * SPAN : (k + 1) * SPAN]

        def g_copy(on):
            nc.vector.tensor_copy(out=g_col[:], in_=g_sb[:])

        pairs = {}

        def pair_tile(kind, first, depth, e, q):
            n = 2 * e + q // 2
            if (kind, n) not in pairs:
                pairs[kind, n] = keep.tile([P, 2, SPAN], F32, name="slot%d" % (first + n % depth), align_bytes=64)
            return pairs[kind, n]

        def mm2(on, e, q):
            c, hf = outs[e]
            bank = next_bank([P, SPAN])
            zt_bank[e, q] = bank
            col = slice(q * P, (q + 1) * P)
            for k in range(2):
                if e in DIRECT:
                    mx(bank[:], h_codes[hf, k][:, col], h_scales[hf, k][:, col], w_codes[2, k, c][:], w_scales[2, k, c][:], k == 0, k == 1)
                else:
                    mx(bank[:], w_codes[2, k, c][:, col], w_scales[2, k, c][:, col], h_codes[hf, k][:], h_scales[hf, k][:], k == 0, k == 1)

        def add_bias(on, e, q):
            c, hf = outs[e]
            zt_sb[e, q] = pair_tile("zt", 0, 4, e, q)[:, q % 2, :]
            bias = b_col[:, 4 * c + q : 4 * c + q + 1]
            if e in DIRECT:
                nc.vector.tensor_tensor(out=zt_sb[e, q], in0=zt_bank[e, q][:], in1=b_wide[c][:], op=ALU.add)
            elif on == "S":
                nc.scalar.activation(out=zt_sb[e, q], in_=zt_bank[e, q][:], func=ACT.Identity, bias=bias)
            else:
                nc.vector.tensor_scalar(out=zt_sb[e, q], in0=zt_bank[e, q][:], scalar1=bias, scalar2=None, op0=ALU.add)

        def turn_back(on, e, r):
            bank = next_bank([P, SPAN])
            z_src[e, r] = bank[:]
            for q in range(4):
                nc.tensor.transpose(bank[:, q * P : (q + 1) * P], zt_sb[e, q][:, r * P : (r + 1) * P], ident[:])

        def part(kind, first, depth, e, r):
            tile = pair_tile(kind, first, depth, e, r)
            return tile[:].rearrange("p a n -> p (a n)") if e in WIDEU else tile[:, r % 2, :]

        def z_of(e, r):
            return part("zt", 0, 4, e, r) if e in DIRECT else z_src[e, r]

        def gate(on, e, r, cols=slice(0, SPAN)):
            nc.scalar.activation(out=part("gate", 4, 2, e, r)[:, cols], in_=z_of(e, r)[:, cols], func=ACT.Relu, bias=half[:], scale=1.0 / 6.0)

        def finish(on, e, r, cols=slice(0, SPAN)):
            nc.vector.scalar_tensor_tensor(out=part("res", 6, 3, e, r)[:, cols], in0=part("gate", 4, 2, e, r)[:, cols], scalar=1.0, in1=z_of(e, r)[:, cols], op0=ALU.min, op1=ALU.mult)

        def store(on, e, r, cols=slice(0, SPAN)):
            c, hf = outs[e]
            i = 4 * hf + r
            nc.sync.dma_start(out=out[i * P : (i + 1) * P, c * SPAN + cols.start : c * SPAN + cols.stop], in_=part("res", 6, 3, e, r)[:, cols])

        outs = OUTS
        h_rows = {}
        b_bank = {}

        by_row = W1_scale.rearrange("(k p j) o -> p k (j o)", p=P, j=PACK)
        nc.scalar.dma_start(out=s0[:], in_=by_row[:, :1])
        load_piece(0)
        nc.sync.dma_start(out=s1[:], in_=by_row[:, 1:])
        load_piece(1)
        load_x(0)
        load_piece(2)
        load_x(1)
        load_piece(3)
        for i in range(2, 8):
            load_x(i)
        nc.sync.dma_start(out=g_sb[:], in_=g.rearrange("(k p j) -> p k j", p=P, j=PACK))
        nc.sync.dma_start(out=s2[:], in_=W2_scale.rearrange("(k p j) o -> p k (j o)", p=P, j=PACK))
        load_piece(4)
        nc.sync.dma_start(out=b_rows[:], in_=b.rearrange("(q n) -> q n", n=P))
        for u in range(5, 8):
            load_piece(u)
        for c in sorted(set(outs[e][0] for e in DIRECT)):
            load_b_wide(c)

        nc.vector.memset(half[:], 0.5)
        make_identity(nc, ident[:])
        nc.gpsimd.memset(b_sq[:], 0.0)
        nc.scalar.activation(out=warm[:], in_=half[:], func=ACT.Relu, bias=half[:])

        def b_copy(on):
            nc.vector.tensor_copy(out=b_sq[: COUT // P, :], in_=b_rows[:])

        def b_turn(on):
            b_bank[0] = next_bank([P, P])
            nc.tensor.transpose(b_bank[0][:], b_sq[:], ident[:])

        def b_columns(on):
            nc.scalar.copy(out=b_col[:], in_=b_bank[0][:, : COUT // P])

        def rows(on, l, c=0, js=range(PACK)):
            for j in js:
                widen(on, l, j, c)

        for l in range(4):
            rows("S", l, 0)
        rows("V", 0, 1)
        rows("V", 1, 1)
        for pair in range(2):
            for i in range(4):
                x_turn("P", i, pair)
        weave("V", 0)
        weave("V", 1)
        rows("V", 2, 1, (0, 1))
        quant_piece("V", 0)
        quant_piece("V", 1)
        weave("V", 2)
        rows("V", 2, 1, (2, 3))
        for i in range(4):
            x_copy("S", i, 0)
        weave("V", 3)
        quant_piece("V", 2)
        for i in range(4):
            x_copy("S", i, 1)
        for i in range(4, 8):
            x_turn("P", i, 0)
        x_quant("V", 0, 0)
        quant_piece("V", 3)
        x_quant("V", 0, 1)
        for t in range(4):
            mm1("P", 0, 0, t)
        weave("S", 4)
        rows("V", 3, 1)
        for i in range(4, 8):
            x_copy("S", i, 0)
            x_turn("P", i, 1)
        weave("SV"[W_ON[3]], 5)
        weave("S", 6)
        weave("SV"[W_ON[0]], 7)
        quant_piece("V", 4)
        g_copy("V")
        quant_piece("V", 7)
        quant_piece("V", 5)
        quant_piece("V", 6)
        b_copy("V")
        rows("V", 4)
        for t in range(4):
            h_scale("S", 0, 0, t)
            mm1("P", 0, 1, t)
        for i in range(4, 8):
            x_copy("S", i, 1)
        x_quant("V", 1, 0)
        x_quant("V", 1, 1)
        rows("V", 5)
        rows("S", 6, 0, range(PACK - V_ROWS[6]))
        for t in range(4):
            mm1("P", 1, 0, t)
            h_scale("S", 0, 1, t)
        b_turn("P")
        h_weave("V", 0, 0)
        weave("SV"[W_ON[2]], 8)
        weave("S", 9)
        h_weave("V", 0, 1)
        weave("SV"[W_ON[1]], 10)
        rows("V", 6, 0, range(PACK - V_ROWS[6], PACK))
        h_quant("V", 0)
        quant_piece("V", 8)
        for t in range(4):
            h_scale("S", 1, 0, t)
            mm1("P", 1, 1, t)
        weave("S", 11)
        b_columns("S")
        for t in range(4):
            mm2("P", 0, t)
            h_scale("S", 1, 1, t)
        h_weave("V", 1, 0)
        quant_piece("V", 10)
        rows("S", 7, 0, range(PACK - V_ROWS[7]))
        for q in range(4):
            add_bias("S", 0, q)
            mm2("P", 1, q)
        h_weave("V", 1, 1)
        rows("V", 7, 0, range(PACK - V_ROWS[7], PACK))
        h_quant("V", 1)
        for e in range(8):
            nxt = e + 1
            for r in range(4):
                if e not in DIRECT:
                    turn_back("P", e, r)
            if e in (0, 2):
                weave("G", 12 + e)
                weave("G", 13 + e)
            for q in range(4):
                if nxt < 8:
                    add_bias("V" if q >= 4 - V_BIAS[nxt] else "S", nxt, q)
            if e + 2 < 8:
                for q in range(4):
                    mm2("P", e + 2, q)
            for r in range(4):
                gate("S", e, r)
                if (e, r) == (7, 3):
                    for cols in (slice(0, SPAN // 2), slice(SPAN // 2, SPAN)):
                        finish("V", e, r, cols)
                        store("D", e, r, cols)
                else:
                    finish("V", e, r)
                    store("D", e, r)
                if r == QAT[min(e // 2, 1)] and e in (1, 3):
                    quant_piece("V", 11 + e)
